import numpy as np, ml_dtypes
CORES = [16,17,18,19,32,33,34,35]
N = 8
BF = ml_dtypes.bfloat16
def gentries(a):
    return np.ascontiguousarray(a.reshape(8, 16, -1).transpose(0, 2, 1)).reshape(8, -1)
def gtable(e):
    e = np.asarray(e); return np.ascontiguousarray(e.reshape(8, -1, 16).transpose(0, 2, 1)).reshape(128, -1).astype(np.int32)
W0, P, S, R, A, W = 3072, 128, 4, 8, 512, 4096
WT = [1, 64, 5, 83, 17, 131, 29, 211, 43, 157, 61, 239, 71, 113, 97, 199]
def parts(rng):
    x = rng.integers(0, 64, (N, 8, 16, W0)); rich = rng.permutation(8)[:3]; x[:, rich] = 48 + (x[:, rich] >> 2)
    fr = rng.integers(0, A, (N, 8, W0))
    hot = np.argsort(rng.random((N, 8, W0)), axis=-1)[..., :256]
    often = np.take_along_axis(hot, rng.integers(0, 256, (N, 8, A * 16)), 2).reshape(N, 8, A, 16)
    C = np.where(rng.random((N, 8, A, 16)) < 0.4, often, rng.integers(0, W0, (N, 8, A, 16)))
    return x, fr, C, rng.integers(0, 64, (N, 8, P, 16)), rng.integers(0, A, (N, 8, P))
def pack(x, fr, C, z, b):
    return {"x0": np.ascontiguousarray(x.reshape(N, 128, W0)).astype(np.float32).astype(BF), "fr0": np.ascontiguousarray(fr).astype(np.int32),
            "pl": np.ascontiguousarray(C.transpose(0, 1, 3, 2).reshape(N, 128, A)).astype(np.int32),
            "z0": np.ascontiguousarray(z.transpose(0, 1, 3, 2).reshape(N, 128, P)).astype(np.float32).astype(BF), "b0": np.stack([gtable(a) for a in b])}
def setup_inputs(rng):
    return pack(*parts(rng))
def setup_inputs_spread(rng):
    x, fr, C, z, b = parts(rng)
    x = (np.exp2(6 * rng.random((N, 8, 1, W0))) * rng.random((N, 8, 16, W0))).astype(np.int64)
    z = (np.exp2(6 * rng.random((N, 8, P, 1))) * rng.random((N, 8, P, 16))).astype(np.int64)
    fr[:, ::2] = (A * rng.random((N, 4, W0)) ** 3).astype(np.int64)
    C = (W0 * rng.random((N, 8, A, 16)) ** 2).astype(np.int64); b = (A * rng.random((N, 8, P)) ** 2).astype(np.int64)
    return pack(x, fr, C, z, b)
def setup_inputs_ends(rng):
    x, fr, C, z, b = parts(rng)
    sd = rng.integers(0, 2, (N, 8, W0)); sd[..., 0] = 0; sd[..., W0 - 1] = 1; sd[:, 7, 1] = 1; fr = sd * (A - 1)
    kd = rng.random((N, 8, 1, W0)); mix = 63 * rng.integers(0, 2, (N, 8, 16, W0))
    less = 63 - (np.arange(16)[:, None] == rng.integers(0, 16, (N, 8, 1, W0)))
    x = np.where(kd < 0.45, 63, np.where(kd < 0.6, less, np.where(kd < 0.75, 0, mix)))
    x[:, 0::2, :, 0] = 0; x[:, 0::2, :, W0 - 1] = 0; x[:, 1::2, :, 0] = 63; x[:, 1::2, :, W0 - 1] = 63
    x[:, 7, :, 1] = 63; x[:, 7, 5, 1] = 62
    ps = rng.integers(0, 2, (N, 8, A)); ps[..., 0] = 0; ps[..., A - 1] = 1; ps = ps[..., None]
    by = np.argsort(sd + 0.5 * rng.random((N, 8, W0)), axis=-1); c1 = np.sum(sd, axis=-1)[:, :, None, None]; u = rng.random((N, 8, A, 16))
    ix = np.where(ps == 1, W0 - c1 + (u * c1).astype(np.int64), (u * (W0 - c1)).astype(np.int64))
    some = np.take_along_axis(by, ix.reshape(N, 8, A * 16), 2).reshape(N, 8, A, 16)
    C = np.where(rng.random((N, 8, A, 16)) < 0.68, ps * (W0 - 1), some)
    kz = rng.random((N, 8, P, 1))
    z = np.where(kz < 0.3, 63, np.where(kz < 0.4, 0, 63 * rng.integers(0, 2, (N, 8, P, 16))))
    b = np.where(rng.random((N, 8, P)) < 0.7, (A - 1) * rng.integers(0, 2, (N, 8, P)), b)
    for a in (A - S, A - 1):
        C[:, 7, a, :15] = 1; C[:, 7, a, 15] = W0 - 1
    z[:, 7, P - 1] = 63; b[:, 7, P - 1] = A - 1
    return pack(x, fr, C, z, b)
def setup_inputs_corners(rng):
    x, fr, C, z, b = parts(rng); o = [int(v) for v in rng.permutation(8)]
    fr[:, o[0]] = (fr[:, o[0]] // N) * N + np.arange(N)[:, None]
    fr[:, o[1]] = int(rng.integers(0, A))
    g = o[2]; zz = rng.integers(0, 64, (N, P, 16)); zz[..., :2] = 0; want = S * np.arange(P)
    need = (want[None, :] - np.sum(zz * np.array(WT), axis=-1)) & (A - 1); zz[..., 0] = need & 63; zz[..., 1] = need >> 6
    x[:, g] = 0; fr[:, g, :A] = np.arange(A); C[:, g, :, 0] = np.arange(A); z[:, g] = zz; b[:, g] = want
    g = o[3]; few = np.argsort(rng.random((N, W0)), axis=-1)[:, :320]; few[:, 0] = 0; few[:, 319] = W0 - 1
    x[:, g] = 63; C[:, g] = np.take_along_axis(few, rng.integers(0, 320, (N, A * 16)), 1).reshape(N, A, 16)
    g = o[4]; C[:, g] = rng.integers(0, W0, (N, A, 1)); C[:, g, ::7] = 0; C[:, g, A - 1] = W0 - 1
    fr[:, g] = rng.integers(0, 8, (N, W0))
    g = o[5]; own = np.arange(A)[:, None] + np.zeros((1, 16), np.int64); kd = rng.integers(0, 4, (N, A, 16))
    C[:, g] = np.where(kd == 0, 0, np.where(kd == 1, W0 - 1, np.where(kd == 2, own, C[:, g])))
    x[:, g] = 63 * rng.integers(0, 2, (N, 1, W0)); b[:, g] = np.where(rng.random((N, P)) < 0.5, np.arange(P) * S, b[:, g])
    g = o[6]; z[:, g, ::2] = 0; z[:, g, 1::2] = 63; x[::2, g] = 0
    g = o[7]; bl = np.arange(P // 4); ev = (bl & 1) == 0; od = ~ev; e8 = np.arange(8); amt = 8 * rng.integers(1, 4, P // 4)
    pt = S * (4 * bl[:, None] + (e8 >> 1)[None, :]) + (e8 & 1)[None, :]
    kind = np.zeros((P // 4, 8, 4), np.int64) + np.array([1, 2, 2, 7, 5, 7, 7, 7])[None, :, None]
    kind[:, 0, 0] = 6; kind[:, 3, 0] = 6; kind[ev, 3, 1] = 3; kind[ev, 4, 0] = 6; kind[ev, 4, 1] = 3; kind[ev, 7, :3] = 3; kind[od, 6, 0] = 3
    nme = np.zeros((A, 4), np.int64); nme[pt] = pt[bl[:, None, None], kind]
    bal = np.zeros((A, 4), np.int64); bal[pt[od, 0], 0] = 2 * amt[od]; bal[pt[od, 3], 0] = amt[od]; bal[pt[od, 6], 0] = amt[od]
    pm = np.argsort(rng.random((N, W0)), axis=-1)[:, :4 * A]; rk = np.arange(N)[:, None]
    fr[rk, g, pm] = nme.reshape(-1)[None, :]; x[:, g] = 0; x[rk, g, 1, pm] = bal.reshape(-1)[None, :]
    C[:, g] = pm[:, 4 * np.arange(A)[:, None] + np.minimum(np.arange(16), 3)[None, :]]
    want = pt[:, [3, 4, 2, 0]].reshape(P); zz = rng.integers(0, 64, (N, P, 16)); zz[..., 0] = 0; zz[..., 10] = 0; zz[..., 1] = np.repeat(amt, 4)
    need = (want[None, :] - np.sum(zz * np.array(WT), axis=-1)) & (A - 1); zz[..., 10] = need // WT[10]; zz[..., 0] = need - WT[10] * zz[..., 10]
    z[:, g] = zz; b[:, g] = want
    return pack(x, fr, C, z, b)
def setup_inputs_crowd(rng):
    x, fr, C, z, b = parts(rng); o = [int(v) for v in rng.permutation(8)]
    for j in (0, 1):
        g = o[j]; one = np.argsort(rng.random((N, W0)), axis=-1)[:, :16]
        fr[:, g] = int(rng.integers(0, A)); x[:, g] = rng.integers(0, 41, (N, 16, W0)); z[:, g] = rng.integers(41, 64, (N, P, 16))
        for r in range(N):
            other = C[r, g, 0].copy(); C[r, g] = one[r]; x[r, g, :, int(one[r, int(rng.integers(0, 16))])] = 63
            if j == 1: C[r, g, S * int(rng.integers(0, P))] = other
    for j in (2, 3):
        g = o[j]; B = int(rng.integers(0, A))
        fr[:, g] = int(rng.integers(0, A)); x[:, g] = rng.integers(0, 41, (N, 16, W0)); z[:, g] = rng.integers(41, 64, (N, P, 16))
        C[:, g] = np.arange(A)[:, None] + A * (np.arange(16)[None, :] % (W0 // A)); x[:, g, :, B] = 63; b[:, g] = B
        if j == 3:
            for r in range(N): b[r, g, int(rng.integers(0, P))] = (B + 1) % A
    g = o[4]; fr[:, g] = (A - 1) * rng.integers(0, 2, (N, W0))
    pay = np.arange(A) // S; pn = np.arange(P); rk = np.arange(N)[:, None]
    for j in (5, 6):
        g = o[j]; bal = np.zeros((A, 4), np.int64)
        if j == 5:
            am = 8 * rng.integers(1, 4, P); nxt = S * ((pn + 1) % P); nme = (S * pay)[:, None] + np.zeros((1, 4), np.int64)
            nme[S * pn, 0] = nxt; nme[S * pn, 1:] = (S * pn + 1)[:, None]; bal[S * pn, 0] = am; bal[S * pn, 1:] = 2 * am[:, None]
            bal[S * pn + 1, 1:] = np.roll(am, 1)[:, None]; want = nxt + 1; z1 = 2 * am
        else:
            bl = np.arange(P // 4); ev = (bl & 1) == 0; am = 8 * rng.integers(1, 3, P // 4); p0, p1, p2, p3 = [S * (4 * bl + v) for v in range(4)]
            nme = np.repeat(np.stack([p0 + 1, p1 + 1, p2, p2 + 1], axis=1).reshape(P), S)[:, None] + np.zeros((1, 4), np.int64)
            up = np.where(ev, p2 + 2 % S, p2 + 1)
            nme[p0, 0] = p1; nme[p1 + 1, 0] = p3 + 1; nme[up, 0] = p3 + 1; nme[p3 + 1] = p1[:, None]
            bal[p0, 0] = 3 * am; bal[p1 + 1, 0] = am; bal[up, 0] = am; bal[p3 + 1, 1:] = 3 * am[:, None]
            want = np.stack([p3 + 1, p0, p0, p1 + 1], axis=1).reshape(P)
            z1 = np.stack([3 * am + np.where(ev, 0, 8), am, am * np.where(ev, 1, 2), am], axis=1).reshape(P)
        pm = np.argsort(rng.random((N, W0)), axis=-1)[:, :4 * A]
        fr[rk, g, pm] = nme.reshape(-1)[None, :]; x[:, g] = 0; x[rk, g, 1, pm] = bal.reshape(-1)[None, :]
        C[:, g] = pm[:, 4 * np.arange(A)[:, None] + np.minimum(np.arange(16), 3)[None, :]]
        zz = rng.integers(0, 64, (N, P, 16)); zz[..., 0] = 0; zz[..., 10] = 0; zz[..., 1] = z1
        need = (want[None, :] - np.sum(zz * np.array(WT), axis=-1)) & (A - 1); zz[..., 10] = need // WT[10]; zz[..., 0] = need - WT[10] * zz[..., 10]
        z[:, g] = zz; b[:, g] = want
    g = o[7]; pm = np.argsort(rng.random((N, W0)), axis=-1)[:, :2 * A]
    nme = np.zeros((A, 2), np.int64); nme[:, 0] = 1; nme[S * pn, 0] = 0; nme[:, 1] = A - 1
    fr[rk, g, pm] = nme.reshape(-1)[None, :]
    for r in range(N):
        x[r, g] = 63 * rng.integers(0, 2, (1, W0)); x[r, g][:, pm[r, 0::2]] = 63; x[r, g][:, pm[r, 1::2]] = 0
    C[:, g] = pm[:, 2 * np.arange(A)[:, None] + (np.arange(16) == 15).astype(np.int64)[None, :]]
    z[:, g] = 63; b[:, g] = S * pn + 1
    return pack(x, fr, C, z, b)
def setup_inputs_ties(rng):
    x, fr, C, z, b = parts(rng)
    x = rng.integers(2, 5, (N, 8, 1, W0)) + np.zeros((1, 1, 16, 1), np.int64); z = rng.integers(2, 4, (N, 8, P, 16)); z[:, :, ::3] = 3
    fr[:, ::2] = rng.integers(0, 24, (N, 4, W0))
    return pack(x, fr, C, z, b)
def check_inputs(d):
    bad = []
    for k, lo, hi in (("x0", 0, 63), ("fr0", 0, A - 1), ("pl", 0, W0 - 1), ("z0", 0, 63), ("b0", 0, A - 1)):
        a = np.asarray(d[k]).astype(np.float64)
        if not (np.min(a) >= lo and np.max(a) <= hi): bad.append("range of " + k)
        elif not np.all(a == np.floor(a)): bad.append("whole numbers in " + k)
    return bad
def first(key):
    ok = np.zeros(len(key), bool); ok[np.unique(key, return_index=True)[1]] = True
    return ok
def reference(x0, fr0, pl, z0, b0):
    X = np.zeros((N, 8, W, 16), np.int32); X[:, :, :W0] = x0.astype(np.float32).astype(np.int32).reshape(N, 8, 16, W0).transpose(0, 1, 3, 2)
    nm = np.zeros((N, 8, W), np.int64); nm[:, :, :W0] = fr0
    sup = np.zeros((N, 8, 2, R * P), np.int64)
    C = np.ascontiguousarray(pl.astype(np.int64).reshape(N, 8, 16, A).transpose(0, 1, 3, 2))
    z = np.ascontiguousarray(z0.astype(np.float32).astype(np.int32).reshape(N, 8, 16, P).transpose(0, 1, 3, 2))
    b = np.stack([gentries(a) for a in b0]).astype(np.int64)
    g2 = np.arange(8)[:, None]; g3 = g2[:, :, None]; pi = np.arange(P)[None, :]; wt = np.array(WT)
    for t in range(R):
        s = t % S; base = X.copy(); took = np.zeros_like(X); back = np.zeros_like(X); D = C.copy(); made = []
        for r in range(N):
            q = (r + 1 + s) % N
            La = C[r][:, s::S]; Ma = C[q][g2, b[r]]
            y = X[r][g3, La]; h = X[q][g3, Ma]
            fk = np.add.reduce(np.minimum(y, z[r][:, :, None, :]), axis=3); hl = np.add.reduce(np.minimum(h, z[r][:, :, None, :]), axis=3)
            fits = nm[r][g3, La][:, :, :, None] == nm[q][g3, Ma][:, :, None, :]
            score = np.where(fits, fk[:, :, :, None] + hl[:, :, None, :], -1).reshape(8, P, 256)
            best = np.argmax(score, axis=2); found = np.max(score, axis=2) >= 0
            k = np.where(found, best >> 4, np.argmin(fk, axis=2)); l = best & 15
            c = La[g2, pi, k]; m = Ma[g2, pi, l]; yk = y[g2, pi, k]
            v = np.minimum(np.minimum(yk, z[r]), h[g2, pi, l])
            gb, ib = np.nonzero(found)
            ok = first(gb * W + c[gb, ib]); gb, ib = gb[ok], ib[ok]
            ok = first(gb * W + m[gb, ib]); gb, ib = gb[ok], ib[ok]
            j = P * t + ib; cb, mb, vb = c[gb, ib], m[gb, ib], v[gb, ib]
            took[r, gb, cb] += vb; took[q, gb, mb] += vb
            made.append((r, gb, W0 + j, vb)); nm[r, gb, W0 + j] = b[r][gb, ib]
            sup[r, gb, 0, j] = cb; sup[r, gb, 1, j] = mb; D[r, gb, S * ib + s, k[gb, ib]] = W0 + j
            gc, ic = np.nonzero(~found & (c >= W0)); n = c[gc, ic] - W0; w = yk[gc, ic]
            base[r, gc, W0 + n] = 0
            np.add.at(back[r], (gc, sup[r, gc, 0, n]), w); np.add.at(back[q], (gc, sup[r, gc, 1, n]), w)
            D[r, gc, S * ic + s, k[gc, ic]] = sup[r, gc, 0, n]
            if t < R - 1:
                z[r] = np.abs(z[r] - yk); b[r] = np.add.reduce(z[r] * wt, axis=2) & (A - 1)
        X = np.minimum(63, np.maximum(base - took, 0) + back); C = D
        for r, gb, n, vb in made: X[r, gb, n] = vb
    rec = np.concatenate([nm[:, :, W0:], sup[:, :, 0], sup[:, :, 1]], axis=1)
    return {"xo": np.ascontiguousarray(X.transpose(0, 1, 3, 2)).reshape(N, 128, W).astype(np.float32).astype(BF),
            "co": np.ascontiguousarray(C.transpose(0, 1, 3, 2)).reshape(N, 128, A).astype(np.float32), "rec": rec.astype(np.float32)}

@@ -1,0 +1,634 @@
+from concourse.mybir import AluOpType, AxisListType, ActivationFunctionType
+
+ALU = AluOpType
+ACT = ActivationFunctionType
+NR = 8
+WT = [1, 64, 5, 83, 17, 131, 29, 211, 43, 157, 61, 239, 71, 113, 97, 199]
+GW = 272
+SW = 8 * GW
+XW = 4224
+ZW = 272
+ROUND = 12582912.0
+HALF = 2047.5
+
+
+def sb(cols, dtype):
+    return ("sbuf", [128, cols], dtype)
+
+
+F32, BF, F16, I32, U16 = "float32", "bfloat16", "float16", "int32", "uint16"
+SCRATCH = {
+    "ps": ("psum", [128, 4096], F32),
+    "X": sb(XW, F32), "NT": sb(3072, BF), "NW": sb(8192, BF), "fri": sb(192, I32), "frb": sb(192, BF),
+    "pli": sb(512, I32), "plu": sb(512, U16), "CN": sb(512, F32), "cnt": sb(512, F32), "cni": sb(512, I32),
+    "cnj": sb(512, I32), "b0i": sb(8, I32), "IOT": sb(4096, F32),
+    "ZS": sb(NR * ZW, BF), "ZL": sb(NR * ZW, BF), "LS": sb(NR * 128, F16), "LL": sb(NR * 256, F16),
+    "FS": sb(NR * 128, F16), "FL": sb(NR * 128, F16), "DS": sb(NR * 144, F32), "DL": sb(NR * 144, F32),
+    "VS": sb(NR * 128, F32), "VL": sb(NR * 128, F32), "QS": sb(NR * 80, U16), "QL": sb(NR * 80, U16),
+    "zxh": sb(2048, BF), "zxf": sb(2048, BF), "ymin": sb(4096, BF), "hmin": sb(4096, BF),
+    "SK": sb(SW, F16), "SN": sb(SW, F16), "SL": sb(SW, F16), "CR": sb(3 * GW, F16), "CL": sb(128, F16),
+    "SG": sb(1024, BF), "TR": sb(512, BF), "EC": sb(1024, BF), "AB": sb(1024, BF),
+    "EM": ("sbuf", [128, 64, 16], BF), "REC": sb(3072, F32),
+    "KI": sb(GW, F32), "LI": sb(GW, F32), "CI": sb(GW, F32), "GI": sb(128, F32), "G8": sb(64, F32), "W8": sb(64, F32),
+    "KP": sb(GW, F16), "KN": sb(GW, F16), "LP": sb(GW, F16), "pint": sb(16, I32), "col": sb(32, F32),
+    "blk": sb(8, F32), "BS8": sb(8, F32), "I17": sb(32, F32), "T1": sb(32, F32), "Zw": sb(144, BF), "Zn": sb(144, BF),
+    "Ib": sb(128, BF), "NIb": sb(128, BF), "I32": sb(128, F32), "NI32": sb(128, F32),
+    "BLK": sb(128, BF), "WB": sb(128, BF), "wrow": sb(16, F32), "wtmp": sb(16, F32), "MD": sb(256, BF),
+    "RST": sb(256, F32), "RS8": sb(64, F32), "WT64": sb(64, F32), "wt2": sb(64, F32), "off7": sb(4, U16),
+    "off8": sb(4, U16), "dum": sb(24, F32), "BASE": sb(64, F32),
+    "Li": sb(128, I32), "La": sb(128, I32), "Lr": sb(128, F32), "Lu": sb(128, U16),
+    "Mi": sb(128, I32), "Ma": sb(128, I32), "Mr": sb(128, F32), "Mu": sb(128, U16), "NM": sb(128, BF),
+    "bfu": sb(8, U16), "HS": sb(128, F16), "U": sb(8, F32), "UX": sb(128, F32), "Ui": sb(8, I32), "dec": sb(32, I32),
+    "offH": sb(8, U16), "klu": sb(16, U16), "LM": sb(256, F16), "r1": sb(8, BF), "r2": sb(8, BF), "sc": sb(256, F32),
+    "V6": sb(48, F32), "DM": sb(NR * 48, F32), "nf": sb(8, F32), "ge": sb(8, F32), "cls": sb(8, F32), "t3": sb(32, F32),
+    "FIN": sb(48, F32), "E64": sb(64, F32), "B64": sb(64, F32), "G48": sb(48, F32),
+    "cu": sb(8, U16), "Bm": sb(128, F32), "yk": sb(128, BF), "su": sb(128, F32), "ui": sb(8, I32),
+    "ub": sb(8, I32), "bhu": sb(NR * 8, U16), "nv": sb(128, F32), "nd": sb(128, F32),
+    "dlt": sb(4 * 128, F32), "dl2": sb(128, F32), "tk": sb(128, F32), "tc": sb(128, F32), "c63": sb(128, F32),
+    "f63": sb(128, F32), "WS": sb(512, F32), "WL": sb(512, F32), "CS": sb(NR * 16, U16), "CD": sb(NR * 8, U16),
+    "blkb": sb(8, BF), "cm": sb(16, F32), "ok": sb(8, I32),
+}
+MSGS = ["z", "l", "f", "d", "v", "q", "c", "w"]
+SEMAPHORES = (["V", "S", "P", "G", "sent", "ld0", "ld1", "ld2", "ld3", "ld4", "ldx", "outg", "outs", "n0"]
+              + [m + str(t) for m in MSGS for t in range(NR)])
+
+
+def rank_program(g, core, T, topo):
+    rank = T.rank_of(core)
+    if rank is None:
+        return
+    n = len(T.cores)
+    queues = {"V": g.vector, "S": g.scalar, "P": g.tensor, "G": g, "Y": g.sync}
+
+    ops = []
+    hist = {}
+    clock = {q: {} for q in queues}
+    seq = {q: 0 for q in queues}
+    marked = {q: set() for q in queues}
+
+    def A(name, lo=0, hi=None, step=1, p=None):
+        t = T[name]
+        if hi is None:
+            hi = t.shape[-1]
+        ps_ = slice(None) if p is None else p
+        ap = t[ps_, lo:hi] if step == 1 else t[ps_, lo:hi:step]
+        return (ap, [(name, lo, hi, step)])
+
+    def IND(win, off):
+        return (win[0].indirect(off[0]), win[1], off[1])
+
+    def P(lo, hi, step=1, p=None):
+        return A("ps", lo, hi, step, p)
+
+    def keys(x):
+        return x[1] if isinstance(x, tuple) else []
+
+    def ap(x):
+        return x[0] if isinstance(x, tuple) else x
+
+    def record(q, fn, reads, writes, token=None):
+        need = {}
+        snaps = []
+        for lst, wr in ((reads, False), (writes, True)):
+            for (name, lo, hi, st) in lst:
+                for e in hist.get(name, []):
+                    elo, ehi, ewr, eq, tok, snap, est = e
+                    over = elo < hi and lo < ehi and not (st == est and (lo - elo) % st)
+                    if name == "ps" and eq != q:
+                        dep = elo // 512 <= (hi - 1) // 512 and lo // 512 <= (ehi - 1) // 512
+                    elif eq == q and q == "P":
+                        dep = False
+                    else:
+                        dep = over and (ewr or wr)
+                    if dep and clock[q].get(tok[0], 0) < tok[1]:
+                        if need.get(tok[0], 0) < tok[1]:
+                            need[tok[0]] = tok[1]
+                        snaps.append((tok, snap))
+        for tok, snap in snaps:
+            for k2, v2 in snap.items():
+                if k2 != tok[0] and need.get(k2, 1 << 30) <= v2:
+                    need.pop(k2)
+        for tok, snap in snaps:
+            for k2, v2 in snap.items():
+                if clock[q].get(k2, 0) < v2:
+                    clock[q][k2] = v2
+        for k2, v2 in need.items():
+            if clock[q].get(k2, 0) < v2:
+                clock[q][k2] = v2
+            if k2 in marked:
+                marked[k2].add(v2)
+        if token is None:
+            seq[q] += 1
+            tok, eq = (q, seq[q]), q
+        else:
+            tok, eq = token, "dma"
+        snap = dict(clock[q])
+        ops.append((q, fn, need, tok, token is None))
+        def covers(lo, hi, st, e):
+            return lo <= e[0] and e[1] <= hi and (st == 1 or (st == e[6] and (lo - e[0]) % st == 0))
+
+        for (name, lo, hi, st) in writes:
+            h = hist.setdefault(name, [])
+            h[:] = [e for e in h if not covers(lo, hi, st, e)]
+            h.append((lo, hi, True, eq, tok, snap, st))
+        for (name, lo, hi, st) in reads:
+            h = hist.setdefault(name, [])
+            h[:] = [e for e in h if not (e[3] == eq and eq != "dma" and not e[2] and covers(lo, hi, st, e))]
+            h.append((lo, hi, False, eq, tok, snap, st))
+
+    def rw(out, ins):
+        r = []
+        for x in ins:
+            r += keys(x)
+            if isinstance(x, tuple) and len(x) == 3:
+                r += x[2]
+        if len(out) == 3:
+            r += out[2]
+        return r, out[1]
+
+    def copy(out, in_):
+        record("V", lambda: g.vector.tensor_copy(ap(out), ap(in_)), *rw(out, [in_]))
+
+    def tt(out, a, b, op):
+        record("V", lambda: g.vector.tensor_tensor(ap(out), ap(a), ap(b), op), *rw(out, [a, b]))
+
+    def ts(out, a, s1, op0, s2=None, op1=None):
+        if op1 is None:
+            record("V", lambda: g.vector.tensor_scalar(ap(out), ap(a), ap(s1), None, op0), *rw(out, [a, s1]))
+        else:
+            record("V", lambda: g.vector.tensor_scalar(ap(out), ap(a), ap(s1), ap(s2), op0, op1), *rw(out, [a, s1, s2]))
+
+    def mset(out, c):
+        record("V", lambda: g.vector.memset(ap(out), c), *rw(out, []))
+
+    def scan(out, d0, d1, op1):
+        record("V", lambda: g.vector.tensor_tensor_scan(ap(out), ap(d0), ap(d1), 0.0, ALU.mult, op1), *rw(out, [d0, d1]))
+
+    def red(out, in_, op, absv):
+        record("V", lambda: g.vector.tensor_reduce(ap(out), ap(in_), AxisListType.X, op, apply_absolute_value=absv),
+               *rw(out, [in_]))
+
+    def act(out, in_, func=ACT.Identity, bias=0.0, scale=1.0):
+        record("S", lambda: g.scalar.activation(ap(out), ap(in_), func, bias=ap(bias), scale=ap(scale)),
+               *rw(out, [in_, bias, scale]))
+
+    def mm(out, lhsT, rhs, start, stop):
+        record("P", lambda: g.tensor.matmul(ap(out), ap(lhsT), ap(rhs), start, stop), *rw(out, [lhsT, rhs]))
+
+    def iota(out, pattern, base, cm, flt=True):
+        if flt:
+            record("G", lambda: g.iota(ap(out), pattern, base, cm, allow_small_or_imprecise_dtypes=True), *rw(out, []))
+        else:
+            record("G", lambda: g.iota(ap(out), pattern, base, cm), *rw(out, []))
+
+    dmacount = {}
+
+    def dma(q, out, in_, sem):
+        dmacount[sem] = dmacount.get(sem, 0) + 16
+        record(q, lambda: queues[q].dma_start(ap(out), ap(in_)), keys(in_), keys(out), token=(sem, dmacount[sem]))
+
+    sent = [0]
+
+    def send(dst_rank, out, in_, sem):
+        dst = T.cores[dst_rank]
+        rid, pid, _se = topo.addr(dst)
+        sent[0] += len(topo.engines(core, dst))
+        record("G", lambda: g.remote_dma(ap(out), ap(in_), T.sem[sem], T.sem["sent"], pid, rid, topo.mask(core, dst)),
+               keys(in_), [], token=("sent", 0))
+
+    def arrive(src_rank, land, sem):
+        tok = (sem, len(topo.engines(T.cores[src_rank], core)))
+        for (name, lo, hi, st) in land[1]:
+            hist.setdefault(name, []).append((lo, hi, True, "dma", tok, {}, st))
+
+    def far(t):
+        return (rank + 1 + t % 4) % n
+
+    def home(t):
+        return (rank - 1 - t % 4) % n
+
+    def qpart(name, t):
+        return A(name, 80 * t + 16, 80 * t + 64) if t < 4 else A(name, 80 * t, 80 * t + 72)
+
+    arrive(home(0), A("ZL", 0, 128), "n0")
+    for t in range(NR):
+        arrive(home(t), A("ZL", ZW * t + (128 if t == 0 else 0), ZW * t + 264), "z%d" % t)
+        arrive(home(t), A("LL", 256 * t, 256 * t + 128), "l%d" % t)
+        arrive(home(t), A("FL", 128 * t, 128 * t + 128), "f%d" % t)
+        arrive(far(t), A("DL", 144 * t, 144 * t + 136), "d%d" % t)
+        arrive(home(t), A("VL", 128 * t, 128 * t + 128), "v%d" % t)
+        arrive(far(t), qpart("QL", t), "q%d" % t)
+        if t < NR - 1:
+            arrive(far(t), A("CD", 8 * t, 8 * t + 8), "c%d" % t)
+        if t >= 4:
+            arrive(home(t), A("WL", 128 * (t - 4), 128 * (t - 3)), "w%d" % t)
+
+    def C(j):
+        return A("col", j, j + 1)
+
+    PC, PM, PG, P16, WC, CA, CBF, CBN, C1, CN1, WE, TA, TB = range(13)
+    B5, B6, B7 = 5 * 512, 6 * 512, 7 * 512
+    Xw = A("X")
+
+    dma("Y", A("fri"), T.fr0[:], "ld0")
+    dma("S", A("pli"), T.pl[:], "ld2")
+    dma("G", A("X", 0, 3072), T.x0[:], "ldx")
+    dma("Y", A("ZS", 128, 256), T.z0[:], "ld1")
+    dma("S", A("b0i"), T.b0[:], "ld3")
+    mset(A("NT"), 0.0)
+    iota(A("pint", 0, 4), [[0, 4]], 0, 1, False)
+    iota(A("CI", 0, 256), [[1, 256]], 0, 0)
+    mset(A("Zw"), 0.0)
+    mset(A("Zn"), 0.0)
+    mset(A("BASE", 32, 64), 0.0)
+    ts(A("pint", 4, 5), A("pint", 0, 1), 15, ALU.bitwise_and)
+    ts(A("pint", 5, 6), A("pint", 0, 1), 4, ALU.arith_shift_right)
+    ts(A("pint", 8, 12), A("pint", 0, 4), 7, ALU.bitwise_and)
+    copy(C(PC), A("pint", 0, 1))
+    copy(A("col", PM, PG + 1), A("pint", 4, 6))
+    mset(A("BASE", 48, 56), 16.0)
+    ts(A("frb"), A("fri"), -256.0, ALU.add)
+    dma("Y", A("NT", p=slice(0, 128, 16)), A("frb"), "ld4")
+    ts(A("ZS", 256, 264), A("b0i"), -256.0, ALU.add)
+    copy(A("bhu", 0, 8), A("b0i"))
+    iota(A("KI", 0, 256), [[1, 16], [0, 16]], 0, 0)
+    iota(A("KI", 256, GW), [[1, 16]], 0, 0)
+    iota(A("LI", 0, 256), [[0, 16], [1, 16]], 0, 0)
+    iota(A("LI", 256, GW), [[0, 16]], -1, 0)
+    send(far(0), A("ZL", 128, 264), A("ZS", 128, 264), "z0")
+    iota(A("X", 3072, XW), [[0, XW - 3072]], 0, 0)
+    iota(A("GI"), [[1, 8], [0, 16]], 0, 0)
+    iota(A("CI", 256, GW), [[-16, 16]], -2048, 0)
+    iota(A("G8"), [[0, 8], [1, 8]], 0, 0)
+    iota(A("W8"), [[-16, 8], [0, 8]], 257, 0)
+    iota(A("dum"), [[0, 3], [16, 8]], 4096, 0)
+    for e in range(16):
+        iota(A("wrow", e, e + 1), [[0, 1]], WT[e], 0)
+
+    def expand(dst, src, k0=0, k1=16):
+        for k in range(k0, k1):
+            act(A(dst, k, 2048, 16), src, ACT.Copy)
+
+    expand("zxh", A("ZS", 128, 256))
+    for s4 in range(4):
+        copy(A("plu", 128 * s4, 128 * s4 + 128), A("pli", s4, 512, 4))
+    ts(A("LS", 0, 128), A("plu", 0, 128), -2048.0, ALU.add)
+    send(far(0), A("LL", 0, 128), A("LS", 0, 128), "l0")
+    ts(A("blk"), A("CI", 0, 8), C(PG), ALU.is_equal)
+    ts(A("off7"), A("pint", 8, 12), 8.0, ALU.mult, 7.0, ALU.add)
+    copy(A("off8"), A("pint", 8, 12))
+    ts(A("Zw", 15, 143, 16), A("blk"), 1.0 / 128, ALU.mult)
+    ts(A("Zn", 15, 143, 16), A("blk"), 4096.0, ALU.mult)
+    ts(A("cnt"), A("pli"), -HALF, ALU.add)
+
+    def names_chunk(ch, eng):
+        src = IND(A("NT"), A("plu", 64 * ch, 64 * ch + 64))
+        out = A("NW", 1024 * ch, 1024 * ch + 1024)
+        if eng == "S":
+            act(out, src, ACT.Copy)
+        else:
+            copy(out, src)
+
+    def fold16(buf, lo, cols, out_lo, w="Zw"):
+        for k in range(16):
+            mm(P(out_lo, out_lo + cols), A(w, 15 - k, 143 - k), A(buf, lo + k, lo + 16 * cols, 16), k == 0, k == 15)
+
+    def fold_names(ch):
+        fold16("NW", 1024 * ch, 64, (B6 if ch < 2 else B7) + 64 * ch, "Zn")
+
+    for ch in range(3):
+        names_chunk(ch, "S")
+    for ch in range(2):
+        fold_names(ch)
+    act(A("ZS", 0, 128), P(B6, B6 + 128), ACT.Identity, 0.0, -1.0 / 64)
+    send(far(0), A("ZL", 0, 128), A("ZS", 0, 128), "n0")
+    iota(A("hmin", 2048, 4096), [[0, 2048]], 63, 0)
+    iota(A("IOT", 0, 512), [[1, 512]], 0, 0)
+    for ch in range(3, 7):
+        names_chunk(ch, "S")
+    for ch in range(2, 4):
+        fold_names(ch)
+
+    ts(A("KP"), A("KI"), C(PM), ALU.is_equal, -128.0, ALU.mult)
+    ts(A("LP"), A("LI"), C(PM), ALU.is_equal, -128.0, ALU.mult)
+    ts(A("KN", 256, GW), A("KI", 256, GW), 0.0, ALU.mult)
+    copy(A("KN", 0, 256), A("KP", 0, 256))
+    for gg in range(8):
+        ts(A("SK", GW * gg, GW * gg + GW), A("KP"), A("blk", gg, gg + 1), ALU.mult)
+        ts(A("SL", GW * gg, GW * gg + GW), A("LP"), A("blk", gg, gg + 1), ALU.mult)
+        ts(A("SN", GW * gg, GW * gg + GW), A("KN"), A("blk", gg, gg + 1), ALU.mult)
+    ts(C(P16), C(PM), 16.0, ALU.mult)
+    ts(C(WC), C(PC), -1.0, ALU.mult, 256.0, ALU.add)
+    ts(C(CA), C(PC), 0.0, ALU.is_equal, 1.0 / 4096, ALU.mult)
+    ts(C(C1), C(PC), 1.0, ALU.is_equal)
+    ts(C(CN1), C(PC), 1.0, ALU.not_equal)
+    ts(C(TA), C(PC), 2.0, ALU.is_equal, 2016.0, ALU.mult)
+    ts(C(TB), C(PC), 2.0, ALU.is_equal, -2017.0, ALU.mult)
+    ts(A("BLK"), A("GI"), C(PG), ALU.is_equal)
+    ts(A("Ib"), A("CI", 0, 128), C(PC), ALU.is_equal)
+    ts(C(CBF), C(C1), 1.0 / 16, ALU.mult, C(TA), ALU.add)
+    ts(C(CBN), C(C1), -1.0 / 16, ALU.mult, C(TB), ALU.add)
+    ts(A("CL"), A("GI"), C(C1), ALU.mult, C(CN1), ALU.add)
+    ts(A("I17"), A("CI", 0, 32), C(PM), ALU.is_equal)
+    ts(A("T1"), A("CI", 0, 32), 16.0, ALU.is_lt)
+    ts(A("BS8"), A("blk"), 4096.0, ALU.mult)
+    ts(A("CR", 0, 256), A("CI", 0, 256), C(CA), ALU.mult, C(CBF), ALU.add)
+    ts(A("CR", 256, GW), A("CI", 256, GW), C(CA), ALU.mult, C(CBN), ALU.add)
+    ts(A("TR", 0, 128), A("CI", 0, 128), C(PC), ALU.is_lt, 0.5, ALU.mult)
+    ts(A("sc", 0, 128), A("LI", 0, 128), C(PM), ALU.is_equal, 133120.0, ALU.mult)
+    copy(A("CR", GW, 2 * GW), A("CR", 0, GW))
+    copy(A("CR", 2 * GW, 3 * GW), A("CR", 0, GW))
+    ts(A("RST"), A("LI", 0, 256), 0.0, ALU.not_equal)
+    ts(A("RS8"), A("G8"), 0.0, ALU.not_equal)
+    ts(A("wt2"), A("G8"), C(PG), ALU.is_equal)
+    ts(A("W8"), A("W8"), C(PM), ALU.subtract)
+    ts(A("dum"), A("dum"), C(PM), ALU.add)
+    tt(A("wtmp"), A("wrow"), A("I17", 0, 16), ALU.mult)
+    tt(A("wt2"), A("wt2"), A("W8"), ALU.mult)
+    copy(A("BASE", 16, 32), A("dum", 0, 16))
+    red(C(WE), A("wtmp"), ALU.add, False)
+    ts(A("WT64"), A("wt2"), -1.0, ALU.add)
+    ts(A("WB"), A("BLK"), C(WE), ALU.mult)
+
+    def late_constants():
+        for gg in range(8):
+            act(A("SG", 128 * gg, 128 * gg + 128), A("BLK"), ACT.Identity, A("blk", gg, gg + 1), 0.0)
+        act(A("blkb"), A("blk"), ACT.Copy)
+        for j in range(2):
+            act(A("MD", 128 * j, 128 * j + 128), A("sc", 0, 128), ACT.Identity, -131072.0, 1.0)
+        for j in range(1, 4):
+            act(A("TR", 128 * j, 128 * j + 128), A("TR", 0, 128), ACT.Copy)
+        act(A("NIb"), A("Ib"), ACT.Identity, 0.0, -1.0)
+        act(A("I32"), A("Ib"), ACT.Copy)
+        act(A("NI32"), A("Ib"), ACT.Identity, 0.0, -1.0)
+        act(A("ymin", 2048, 4096), A("hmin", 2048, 4096), ACT.Copy)
+
+    banks = [(0, 512), (512, 1024), (1024, 1536), (1536, 2048), (2048, SW)]
+
+    def spass(lhsT, sel, start, stop, which=banks):
+        for lo, hi in which:
+            mm(P(lo, hi), lhsT, A(sel, lo, hi), start, stop)
+
+    def ccol(t):
+        return A("CN", t % 4, 512, 4)
+
+    def lnames(t):
+        act(A("Lr"), ccol(t), ACT.Identity, ROUND, 1.0 / 4096)
+        act(A("ZS", ZW * t, ZW * t + 128), A("Lr"), ACT.Identity, 64.0 * ROUND, -64.0)
+
+    def lprep(t):
+        ts(A("Li"), ccol(t), HALF, ALU.add)
+        ts(A("La"), A("Li"), 4095, ALU.bitwise_and)
+        copy(A("Lu"), A("La"))
+        ts(A("LS", 128 * t, 128 * t + 128), A("Lu"), -2048.0, ALU.add)
+        send(far(t), A("LL", 256 * t, 256 * t + 128), A("LS", 128 * t, 128 * t + 128), "l%d" % t)
+
+    def lists(t):
+        q0 = 80 * t
+        d = A("dlt", 128 * t, 128 * t + 128) if t < 4 else A("dl2")
+        reg = P(B7 + 256, B7 + 384)
+        mm(reg, A("I32"), ccol(t), True, False)
+        tt(d, IND(A("I17"), A("QL", q0 + 48, q0 + 56)), A("nd"), ALU.mult)
+        if t >= 4:
+            tt(A("tc"), IND(A("IOT", 0, 16), A("QL", q0 + 64, q0 + 72)), A("dlt", 128 * (t - 4), 128 * (t - 3)), ALU.mult)
+        mm(reg, A("I32"), d, False, t < 4)
+        if t >= 4:
+            mm(reg, A("NI32"), A("tc"), False, True)
+        act(ccol(t), reg, ACT.Copy)
+
+    def entries(t):
+        tt(A("X", 3072 + 128 * t, 3200 + 128 * t), IND(A("T1"), A("QL", 80 * t + 48, 80 * t + 56)),
+           A("VS", 128 * t, 128 * t + 128), ALU.mult)
+
+    def records(t):
+        q0 = 80 * t
+        for j, o in ((0, 56), (1, 32), (2, 40)):
+            act(A("REC", 1024 * j + 128 * t, 1024 * j + 128 * t + 128), IND(A("IOT"), A("QL", q0 + o, q0 + o + 8)), ACT.Copy)
+
+    def mprep(t):
+        ts(A("Mi"), IND(A("CN"), A("bfu")), HALF, ALU.add)
+        act(A("Mr"), IND(A("CN"), A("bfu")), ACT.Identity, ROUND, 1.0 / 4096)
+        act(A("NM"), A("Mr"), ACT.Identity, -64.0 * ROUND, 64.0)
+        ts(A("Ma"), A("Mi"), 4095, ALU.bitwise_and)
+        copy(A("Mu"), A("Ma"))
+
+    def gmin(out, offs, zx, h, wide):
+        tt(A(out, 1024 * h, 1024 * h + 1024), IND(A("X", 0, wide), A(offs, 64 * h, 64 * h + 64)),
+           A(zx, 1024 * h, 1024 * h + 1024), ALU.min)
+
+    for t in range(NR):
+        yw = 3072 + 128 * max(0, t - 3)
+        z0_, l0, d0, q0 = ZW * t, 256 * t, 144 * t, 80 * t
+        vs = A("VS", 128 * t, 128 * t + 128)
+        vl = A("VL", 128 * t, 128 * t + 128)
+        zl = A("ZL", z0_ + 128, z0_ + 256)
+        bl = A("ZL", z0_ + 256, z0_ + 264)
+        fs, fl = A("FS", 128 * t, 128 * t + 128), A("FL", 128 * t, 128 * t + 128)
+        if t > 0:
+            lists(t - 1)
+            spass(A("ZL", z0_, z0_ + 128), "SN", True, False)
+            gmin("ymin", "Lu", "zxh", 0, yw)
+            fold16("ymin", 0, 64, B5)
+            ts(A("bfu"), bl, 256.0, ALU.add)
+            mprep(t)
+            expand("zxf", zl)
+            spass(A("NM"), "SL", False, False)
+            gmin("ymin", "Lu", "zxh", 1, yw)
+            fold16("ymin", 1024, 64, B5 + 64)
+            entries(t - 1)
+            ts(A("LL", l0 + 128, l0 + 256), A("Mu"), -2048.0, ALU.add)
+            copy(fs, P(B5, B5 + 128))
+            send(far(t), fl, fs, "f%d" % t)
+            records(t - 1)
+        else:
+            for h in range(2):
+                gmin("ymin", "plu", "zxh", h, yw)
+                fold16("ymin", 1024 * h, 64, B5 + 64 * h)
+                fold_names(4 + h)
+            ts(A("bfu"), bl, 256.0, ALU.add)
+            names_chunk(7, "V")
+            copy(fs, P(B5, B5 + 128))
+            send(far(t), fl, fs, "f%d" % t)
+            expand("zxf", zl)
+            for ch in (6, 7):
+                fold_names(ch)
+            spass(A("ZL", 0, 128), "SN", True, False)
+            for s4 in range(4):
+                lo = (B6 if s4 == 0 else B7) + 128 * s4
+                tt(ccol(s4), P(lo, lo + 128), A("cnt", s4, 512, 4), ALU.add)
+            mprep(0)
+            ts(A("LL", l0 + 128, l0 + 256), A("Mu"), -2048.0, ALU.add)
+            late_constants()
+            iota(A("IOT", 512, 4096), [[1, 3584]], 512, 0)
+            spass(A("NM"), "SL", False, False)
+        act(A("nv"), IND(A("IOT", 0, 512), A("bhu", 8 * t, 8 * t + 8)), ACT.Identity, -256.0 * 4096 - HALF, 4096.0)
+        if t >= 4:
+            ws, wl = A("WS", 128 * (t - 4), 128 * (t - 3)), A("WL", 128 * (t - 4), 128 * (t - 3))
+            act(ws, A("X", 3072 + 128 * (t - 4), 3072 + 128 * (t - 3)), ACT.Copy)
+            send(far(t), wl, ws, "w%d" % t)
+            act(A("c63"), ws, ACT.Identity, 63.0, -1.0)
+        if t < NR - 1:
+            lnames(t + 1)
+        if t >= 4:
+            act(A("f63"), wl, ACT.Identity, 63.0, -1.0)
+        for lo, hi in banks:
+            mm(P(lo, hi), A("CL", p=slice(0, 3)), A("CR", lo % GW, lo % GW + hi - lo, p=slice(0, 3)), False, False)
+        for h in range(2):
+            gmin("hmin", "Mu", "zxf", h, XW)
+            if h == 1:
+                spass(fl, "SK", False, False, banks[0:2])
+            fold16("hmin", 1024 * h, 64, B6 + 64 * h)
+        spass(fl, "SK", False, False, banks[2:3])
+        copy(A("HS"), P(B6, B6 + 128))
+        spass(A("HS"), "SL", False, True, banks[0:3])
+        for b in (3, 4):
+            spass(fl, "SK", False, False, banks[b:b + 1])
+            spass(A("HS"), "SL", False, True, banks[b:b + 1])
+        for gg in range(8):
+            red(A("U", gg, gg + 1), P(GW * gg, GW * gg + GW), ALU.min, True)
+            if gg < 7:
+                act(A("UX", 16 * gg, 16 * gg + 16), A("I17", 0, 16), ACT.Identity, 0.0, A("U", gg, gg + 1))
+        ts(A("UX", 112, 128), A("I17", 0, 16), A("U", 7, 8), ALU.mult)
+        mm(P(B6, B6 + 256), A("Ib"), A("MD"), True, False)
+        for b in range(3):
+            mm(P(512 * b, 512 * b + 512), A("Ib"), A("TR"), True, False)
+        mm(P(B5, B5 + 8), A("UX"), A("BS8"), True, True)
+        for b in (3, 4):
+            mm(P(512 * b, 512 * b + 256), A("Ib"), A("TR", 0, 256), True, False)
+        ts(A("r1"), A("U"), 2017.0, ALU.is_lt, C(WC), ALU.mult)
+        ts(A("V6", 40, 48), bl, 256.0, ALU.add)
+        copy(A("Ui"), P(B5, B5 + 8))
+        ts(A("dec", 16, 24), A("Ui"), 0xF0F, ALU.bitwise_and)
+        ts(A("dec", 0, 8), A("Ui"), 4, ALU.logical_shift_right, 15, ALU.bitwise_and)
+        ts(A("dec", 24, 32), A("Ui"), 0xF00, ALU.bitwise_and)
+        ts(A("offH"), A("dec", 16, 24), C(P16), ALU.add)
+        ts(A("dec", 8, 16), A("Ui"), 15, ALU.bitwise_and)
+        tt(A("ok"), A("dec", 24, 32), A("dec", 0, 8), ALU.add)
+        copy(A("klu"), A("dec", 0, 16))
+        ts(A("DS", d0 + 128, d0 + 136), A("ok"), C(P16), ALU.add)
+        act(A("DS", d0, d0 + 128), IND(A("hmin"), A("offH")), ACT.Copy)
+        send(home(t), A("DL", d0, d0 + 136), A("DS", d0, d0 + 136), "d%d" % t)
+        tt(A("LM"), IND(A("I17"), A("klu")), A("LL", l0, l0 + 256), ALU.mult)
+        for j in range(2):
+            mm(P(B5 + 64 + 8 * j, B5 + 72 + 8 * j), A("LM", 128 * j, 128 * j + 128), A("blkb"), True, True)
+
+        def dpos(j, gg):
+            return 128 * gg if j == 0 else 1024 + 128 * gg + (256 if gg >= 6 else 0)
+
+        def spread(j, g0, g1):
+            for gg in range(g0, g1):
+                mm(P(dpos(j, gg), dpos(j, gg) + 128), A("SG", 128 * gg, 128 * gg + 128), A("LM", 128 * j, 128 * j + 128),
+                   False, gg == g1 - 1)
+
+        def emrows(gg):
+            return (T.EM[:, gg:64:8, :], [("EM", gg, gg + 1, 1)])
+
+        mm(P(B6, B6 + 256), A("BLK"), A("LM"), False, True)
+        spread(1, 0, 4)
+        spread(0, 0, 4)
+        spread(0, 4, 8)
+        spread(1, 4, 6)
+        spread(1, 6, 8)
+        copy(A("V6", 32, 40), A("dec", 0, 8))
+        if t >= 4:
+            ts(A("nf"), A("Ui"), 2017.0 * 4096, ALU.is_ge)
+        copy(A("cm"), P(B5 + 64, B5 + 80))
+        scan(A("sc"), A("RST"), P(B6, B6 + 256), ALU.max)
+        copy(A("CS", 16 * t, 16 * t + 16), A("sc", 15, 256, 16))
+        if t < NR - 1:
+            send(home(t), A("CD", 8 * t, 8 * t + 8), A("CS", 16 * t, 16 * t + 8), "c%d" % t)
+        for g0, g1 in ((0, 4), (4, 6)):
+            for gg in range(g0, g1):
+                act(A("AB", 128 * gg, 128 * gg + 128), P(dpos(1, gg), dpos(1, gg) + 128), ACT.Abs, A("cm", 8 + gg, 9 + gg), -1.0)
+            for gg in range(g0, g1):
+                act(emrows(gg), A("AB", 128 * gg, 128 * gg + 128), ACT.Relu, 1.0, -2.0)
+        for gg in range(8):
+            ts(A("EC", 128 * gg, 128 * gg + 128), P(128 * gg, 128 * gg + 128), A("cm", gg, gg + 1), ALU.is_equal)
+            mm(P(B7 + gg, B7 + gg + 1), A("EC", 128 * gg, 128 * gg + 128), A("r1", gg, gg + 1), True, True)
+        for gg in (6, 7):
+            ts(emrows(gg), P(dpos(1, gg), dpos(1, gg) + 128), A("cm", 8 + gg, 9 + gg), ALU.is_equal)
+        ts(A("r2"), P(B7, B7 + 8), C(WC), ALU.is_equal, C(WC), ALU.mult)
+        for c in range(8):
+            mm(P(B5 + 8 * c, B5 + 8 * c + 8), (T.EM[:, 8 * c:8 * c + 8, :], [("EM", 0, 8, 1)]), A("r2"), True, True)
+        act(A("V6", 0, 16), A("sc", 15, 256, 16), ACT.Copy)
+        act(A("V6", 16, 32), A("sc", 15, 256, 16), ACT.Copy)
+        act(A("Bm"), IND(Xw, A("CS", 16 * t + 8, 16 * t + 16)), ACT.Copy)
+        if t >= 4:
+            p0 = 48 * (t - 4)
+            ts(A("ge"), A("sc", 15, 128, 16), 3072.0, ALU.is_ge)
+            tt(A("DM", p0 + 16, p0 + 24), A("sc", 15, 128, 16), A("dum", 0, 8), ALU.subtract)
+            tt(A("cls"), A("nf"), A("ge"), ALU.mult)
+            tt(A("t3"), IND(A("cls"), A("off8", 0, 2)), A("DM", p0, p0 + 32), ALU.mult)
+            copy(A("QS", q0 + 64, q0 + 72), A("cls"))
+            tt(A("BASE", 0, 24), A("t3", 0, 24), A("dum"), ALU.add)
+            copy(A("QS", q0, q0 + 16), A("BASE", 0, 16))
+        tt(A("DM", 48 * t, 48 * t + 48), A("V6"), A("BASE", 16, 64), ALU.subtract)
+        copy(A("cu"), A("DL", d0 + 128, d0 + 136))
+        tt(A("E64"), P(B5, B5 + 64), A("WT64"), ALU.is_equal)
+        tt(vs, IND(A("ymin"), A("cu")), A("DL", d0, d0 + 128), ALU.min)
+        send(far(t), vl, vs, "v%d" % t)
+        scan(A("B64"), A("RS8"), A("E64"), ALU.add)
+        tt(A("G48"), IND(A("B64"), A("off7", 0, 3)), A("DM", 48 * t, 48 * t + 48), ALU.mult)
+        tt(A("FIN"), A("G48"), A("BASE", 16, 64), ALU.add)
+        copy(A("QS", q0 + 16, q0 + 64), A("FIN"))
+        send(home(t), qpart("QL", t), qpart("QS", t), "q%d" % t)
+        if t < NR - 1:
+            z1 = z0_ + ZW
+            act(A("yk"), IND(Xw, A("CD", 8 * t, 8 * t + 8)), ACT.Copy)
+            reg = P(B7 + 384, B7 + 512)
+            mm(reg, A("NIb"), A("ZS", z0_ + 128, z0_ + 256), True, False)
+            mm(reg, A("Ib"), A("yk"), False, True)
+            act(A("ZS", z1 + 128, z1 + 256), reg, ACT.Abs)
+            mm(P(B6, B6 + 128), A("Ib"), A("MD", 0, 128), True, False)
+            mm(P(B6, B6 + 128), A("WB"), A("ZS", z1 + 128, z1 + 256), False, True)
+            lprep(t + 1)
+            scan(A("su"), A("RST", 0, 128), P(B6, B6 + 128), ALU.max)
+            copy(A("ui"), A("su", 15, 128, 16))
+            ts(A("ub"), A("ui"), 511, ALU.bitwise_and)
+            ts(A("ZS", z1 + 256, z1 + 264), A("ub"), -256.0, ALU.add)
+            send(far(t + 1), A("ZL", z1, z1 + 264), A("ZS", z1, z1 + 264), "z%d" % (t + 1))
+            copy(A("bhu", 8 * t + 8, 8 * t + 16), A("ub"))
+        reg = P(B7 + 128, B7 + 256)
+        mm(reg, A("I32"), A("nv"), True, False)
+        mm(reg, A("I32"), A("IOT", 3072 + 128 * t, 3200 + 128 * t), False, False)
+        mm(reg, A("NI32"), ccol(t), False, True)
+        if t < NR - 1:
+            expand("zxh", A("ZS", z1 + 128, z1 + 256))
+        act(A("nd"), reg, ACT.Copy)
+        tt(IND(Xw, A("QS", q0 + 24, q0 + 32)), A("Bm"), vl, ALU.subtract)
+        oc = A("QL", q0 + 16, q0 + 24)
+        tt(A("tk"), IND(Xw, oc), vs, ALU.max)
+        tt(IND(Xw, oc), A("tk"), vs, ALU.subtract)
+        if t >= 4:
+            for off, cap, w in ((A("QL", q0, q0 + 8), A("c63"), ws), (A("QS", q0 + 8, q0 + 16), A("f63"), wl)):
+                tt(A("tk"), IND(Xw, off), cap, ALU.min)
+                tt(IND(Xw, off), A("tk"), w, ALU.add)
+
+    dma("G", (T.xo[:, 0:3968], []), A("X", 0, 3968), "outg")
+    lists(NR - 1)
+    entries(NR - 1)
+    records(NR - 1)
+    dma("G", (T.xo[:, 3968:4096], []), A("X", 3968, 4096), "outg")
+    ts(A("cni"), A("CN"), HALF, ALU.add)
+    ts(A("cnj"), A("cni"), 4095, ALU.bitwise_and)
+    copy(A("cnt"), A("cnj"))
+    for j in range(3):
+        dma("Y", (T.rec[8 * j:8 * j + 8, :], []), A("REC", 1024 * j, 1024 * j + 1024, p=slice(0, 128, 16)), "outs")
+    dma("Y", (T.co[:], []), A("cnt"), "outs")
+
+    value = {}
+    for q in marked:
+        for j, s in enumerate(sorted(marked[q])):
+            value[(q, s)] = j + 1
+    for q, fn, need, tok, compute in ops:
+        for k2, v2 in need.items():
+            queues[q].wait_ge(T.sem[k2], value[(k2, v2)] if k2 in marked else v2)
+        ins = fn()
+        if compute:
+            if tok in value:
+                ins.then_inc(T.sem[q], 1)
+        elif tok[0] != "sent":
+            ins.then_inc(T.sem[tok[0]], 16)
+    g.wait_ge(T.sem["sent"], sent[0])
+    g.wait_ge(T.sem["outg"], dmacount["outg"])
+    g.sync.wait_ge(T.sem["outs"], dmacount["outs"])

@@ -6,10 +6,15 @@ NR = 8
 WT = [1, 64, 5, 83, 17, 131, 29, 211, 43, 157, 61, 239, 71, 113, 97, 199]
 GW = 272
 SW = 8 * GW
-XW = 4224
-ZW = 272
+SH = 128
+E0 = SH + 3072
+XW = SH + 4096
+MID = SH + 2048
+ZW = 144
 ROUND = 12582912.0
-HALF = 2047.5
+HALF = 4095.5
+BIG = 16384.0
+HUGE = 1073741824.0
 
 
 def sb(cols, dtype):
@@ -19,37 +24,35 @@ def sb(cols, dtype):
 F32, BF, F16, I32, U16 = "float32", "bfloat16", "float16", "int32", "uint16"
 SCRATCH = {
     "ps": ("psum", [128, 4096], F32),
-    "X": sb(XW, F32), "NT": sb(3072, BF), "NW": sb(8192, BF), "fri": sb(192, I32), "frb": sb(192, BF),
-    "pli": sb(512, I32), "plu": sb(512, U16), "CN": sb(512, F32), "cnt": sb(512, F32), "cni": sb(512, I32),
-    "cnj": sb(512, I32), "b0i": sb(8, I32), "IOT": sb(4096, F32),
-    "ZS": sb(NR * ZW, BF), "ZL": sb(NR * ZW, BF), "LS": sb(NR * 128, F16), "LL": sb(NR * 256, F16),
-    "FS": sb(NR * 128, F16), "FL": sb(NR * 128, F16), "DS": sb(NR * 144, F32), "DL": sb(NR * 144, F32),
-    "VS": sb(NR * 128, F32), "VL": sb(NR * 128, F32), "QS": sb(NR * 80, U16), "QL": sb(NR * 80, U16),
-    "zxh": sb(2048, BF), "zxf": sb(2048, BF), "ymin": sb(4096, BF), "hmin": sb(4096, BF),
-    "SK": sb(SW, F16), "SN": sb(SW, F16), "SL": sb(SW, F16), "CR": sb(3 * GW, F16), "CL": sb(128, F16),
-    "SG": sb(1024, BF), "TR": sb(512, BF), "EC": sb(1024, BF), "AB": sb(1024, BF),
+    "X": sb(XW, BF), "NT": sb(E0, BF), "NW": sb(8192, BF), "fri": sb(192, I32), "frb": sb(192, BF),
+    "pli": sb(512, I32), "plu": sb(512, U16), "CN": sb(512, F32), "cnt": sb(512, F32), "b0i": sb(8, I32), "IOT": sb(XW, F32),
+    "ZS": sb(NR * ZW, BF), "ZL": sb(NR * ZW, BF), "NS": sb(NR * 128, BF), "NL": sb(NR * 128, BF),
+    "MS": sb(NR * ZW, F16), "ML": sb(NR * ZW, F16), "HS": sb(NR * 128, F16), "HL": sb(NR * 128, F16),
+    "BS": sb(NR * ZW, F32), "BL": sb(NR * ZW, F32), "VS": sb(NR * 128, BF), "VL": sb(NR * 128, BF),
+    "DS": sb(NR * 8, U16), "DL": sb(NR * 8, U16), "EL": sb(NR * 8, U16), "Q": sb(NR * 56, U16), "FIN": sb(NR * 72, F32),
+    "zxf": sb(2048, BF), "ybuf": sb(2048, BF), "rbuf": sb(2048, BF), "hmin": sb(4096, BF), "OHW": sb(4096, BF),
+    "EXP": sb(2048, BF), "SK": sb(SW, BF), "SN": sb(SW, BF), "SL": sb(SW, BF),
+    "SG": sb(1024, BF), "TR": sb(512, BF), "EC": sb(1024, BF), "AB": sb(512, BF),
     "EM": ("sbuf", [128, 64, 16], BF), "REC": sb(3072, F32),
-    "KI": sb(GW, F32), "LI": sb(GW, F32), "CI": sb(GW, F32), "GI": sb(128, F32), "G8": sb(64, F32), "W8": sb(64, F32),
-    "KP": sb(GW, F16), "KN": sb(GW, F16), "LP": sb(GW, F16), "pint": sb(16, I32), "col": sb(32, F32),
-    "blk": sb(8, F32), "BS8": sb(8, F32), "I17": sb(32, F32), "T1": sb(32, F32), "Zw": sb(144, BF), "Zn": sb(144, BF),
-    "Ib": sb(128, BF), "NIb": sb(128, BF), "I32": sb(128, F32), "NI32": sb(128, F32),
-    "BLK": sb(128, BF), "WB": sb(128, BF), "wrow": sb(16, F32), "wtmp": sb(16, F32), "MD": sb(256, BF),
-    "RST": sb(256, F32), "RS8": sb(64, F32), "WT64": sb(64, F32), "wt2": sb(64, F32), "off7": sb(4, U16),
-    "off8": sb(4, U16), "dum": sb(24, F32), "BASE": sb(64, F32),
-    "Li": sb(128, I32), "La": sb(128, I32), "Lr": sb(128, F32), "Lu": sb(128, U16),
-    "Mi": sb(128, I32), "Ma": sb(128, I32), "Mr": sb(128, F32), "Mu": sb(128, U16), "NM": sb(128, BF),
-    "bfu": sb(8, U16), "HS": sb(128, F16), "U": sb(8, F32), "UX": sb(128, F32), "Ui": sb(8, I32), "dec": sb(32, I32),
-    "offH": sb(8, U16), "klu": sb(16, U16), "LM": sb(256, F16), "r1": sb(8, BF), "r2": sb(8, BF), "sc": sb(256, F32),
-    "V6": sb(48, F32), "DM": sb(NR * 48, F32), "nf": sb(8, F32), "ge": sb(8, F32), "cls": sb(8, F32), "t3": sb(32, F32),
-    "FIN": sb(48, F32), "E64": sb(64, F32), "B64": sb(64, F32), "G48": sb(48, F32),
-    "cu": sb(8, U16), "Bm": sb(128, F32), "yk": sb(128, BF), "su": sb(128, F32), "ui": sb(8, I32),
-    "ub": sb(8, I32), "bhu": sb(NR * 8, U16), "nv": sb(128, F32), "nd": sb(128, F32),
-    "dlt": sb(4 * 128, F32), "dl2": sb(128, F32), "tk": sb(128, F32), "tc": sb(128, F32), "c63": sb(128, F32),
-    "f63": sb(128, F32), "WS": sb(512, F32), "WL": sb(512, F32), "CS": sb(NR * 16, U16), "CD": sb(NR * 8, U16),
-    "blkb": sb(8, BF), "cm": sb(16, F32), "ok": sb(8, I32),
+    "KI": sb(GW, F32), "LI": sb(GW, F32), "CI": sb(GW, F32), "GI": sb(128, F32),
+    "KP": sb(GW, BF), "KN": sb(GW, BF), "LP": sb(GW, BF), "KA": sb(GW, BF), "KB": sb(GW, BF), "CR": sb(GW, BF),
+    "pint": sb(16, I32), "col": sb(32, F32), "blk": sb(8, F32), "blkA": sb(8, F32), "blkb": sb(8, BF), "BS8": sb(8, F32),
+    "I16": sb(16, F32), "Zw": sb(144, BF), "Zn": sb(144, BF), "BLK": sb(128, BF), "WB": sb(128, BF),
+    "MD": sb(256, BF), "RST": sb(256, F32), "sc": sb(256, F32), "su": sb(128, F32),
+    "Ib": sb(128, BF), "NIb": sb(128, BF), "I32": sb(128, F32), "I128": sb(128, BF), "CIb": sb(128, BF),
+    "uf": sb(8, I32), "ubf": sb(8, I32), "wrow": sb(16, F32), "wtmp": sb(16, F32),
+    "off8": sb(4, U16), "JC": sb(16, F32), "iG": sb(8, F32), "BASE": sb(56, F32), "PB": sb(56, F32), "AT": sb(48, F32),
+    "G48": sb(48, F32), "G32": sb(32, F32), "PRE": sb(136, F32), "D1": sb(136, F32), "SC": sb(136, F32), "T2": sb(GW, BF),
+    "NDW": sb(4 * GW, F32), "Li": sb(128, I32), "La": sb(128, I32), "Lr": sb(128, F32), "Lu": sb(256, U16), "L16": sb(256, F16),
+    "NH": sb(128, BF), "Mi": sb(128, I32), "Ma": sb(128, I32), "Mr": sb(128, F32), "Mu": sb(128, U16),
+    "bfu": sb(8, U16), "FT": sb(256, F16), "U": sb(8, F32), "UX": sb(128, F32), "Ui": sb(8, I32), "dec": sb(16, I32),
+    "OF": sb(16, U16), "LM": sb(256, F16), "r1": sb(8, BF), "r2": sb(16, BF), "cm": sb(16, F32),
+    "nfb": sb(8, F32), "cn": sb(8, F32), "cls": sb(8, F32), "flag": sb(8, F32), "cu": sb(8, U16), "ykb": sb(128, BF),
+    "zT": sb(128, BF), "bu": sb(8, U16), "nv": sb(128, BF), "OHk": sb(128, F32),
+    "dl": sb(128, F32), "tk": sb(128, BF), "nvf": sb(128, BF), "nvh": sb(128, BF), "capf": sb(128, BF), "caph": sb(128, BF),
 }
-MSGS = ["z", "l", "f", "d", "v", "q", "c", "w"]
-SEMAPHORES = (["V", "S", "P", "G", "sent", "ld0", "ld1", "ld2", "ld3", "ld4", "ldx", "outg", "outs", "n0"]
+MSGS = ["z", "n", "m", "h", "y", "v", "d", "e"]
+SEMAPHORES = (["V", "S", "P", "G", "sent", "ld0", "ld1", "ld2", "ld3", "ld4", "ld5", "ldx", "outs"]
               + [m + str(t) for m in MSGS for t in range(NR)])
 
 
@@ -64,15 +67,15 @@ def rank_program(g, core, T, topo):
     hist = {}
     clock = {q: {} for q in queues}
     seq = {q: 0 for q in queues}
-    marked = {q: set() for q in queues}
+    marked = {q: set() for q in queues if q != "Y"}
 
     def A(name, lo=0, hi=None, step=1, p=None):
         t = T[name]
         if hi is None:
             hi = t.shape[-1]
         ps_ = slice(None) if p is None else p
-        ap = t[ps_, lo:hi] if step == 1 else t[ps_, lo:hi:step]
-        return (ap, [(name, lo, hi, step)])
+        ap_ = t[ps_, lo:hi] if step == 1 else t[ps_, lo:hi:step]
+        return (ap_, [(name, lo, hi, step)])
 
     def IND(win, off):
         return (win[0].indirect(off[0]), win[1], off[1])
@@ -124,6 +127,7 @@ def rank_program(g, core, T, topo):
             tok, eq = token, "dma"
         snap = dict(clock[q])
         ops.append((q, fn, need, tok, token is None))
+
         def covers(lo, hi, st, e):
             return lo <= e[0] and e[1] <= hi and (st == 1 or (st == e[6] and (lo - e[0]) % st == 0))
 
@@ -161,8 +165,8 @@ def rank_program(g, core, T, topo):
     def mset(out, c):
         record("V", lambda: g.vector.memset(ap(out), c), *rw(out, []))
 
-    def scan(out, d0, d1, op1):
-        record("V", lambda: g.vector.tensor_tensor_scan(ap(out), ap(d0), ap(d1), 0.0, ALU.mult, op1), *rw(out, [d0, d1]))
+    def scan(out, d0, d1, op0, op1):
+        record("V", lambda: g.vector.tensor_tensor_scan(ap(out), ap(d0), ap(d1), 0.0, op0, op1), *rw(out, [d0, d1]))
 
     def red(out, in_, op, absv):
         record("V", lambda: g.vector.tensor_reduce(ap(out), ap(in_), AxisListType.X, op, apply_absolute_value=absv),
@@ -207,81 +211,118 @@ def rank_program(g, core, T, topo):
     def home(t):
         return (rank - 1 - t % 4) % n
 
-    def qpart(name, t):
-        return A(name, 80 * t + 16, 80 * t + 64) if t < 4 else A(name, 80 * t, 80 * t + 72)
+    def R(name, t, w=128, lo=0, hi=None):
+        return A(name, w * t + lo, w * t + (w if hi is None else hi))
 
-    arrive(home(0), A("ZL", 0, 128), "n0")
     for t in range(NR):
-        arrive(home(t), A("ZL", ZW * t + (128 if t == 0 else 0), ZW * t + 264), "z%d" % t)
-        arrive(home(t), A("LL", 256 * t, 256 * t + 128), "l%d" % t)
-        arrive(home(t), A("FL", 128 * t, 128 * t + 128), "f%d" % t)
-        arrive(far(t), A("DL", 144 * t, 144 * t + 136), "d%d" % t)
-        arrive(home(t), A("VL", 128 * t, 128 * t + 128), "v%d" % t)
-        arrive(far(t), qpart("QL", t), "q%d" % t)
-        if t < NR - 1:
-            arrive(far(t), A("CD", 8 * t, 8 * t + 8), "c%d" % t)
+        arrive(home(t), R("ZL", t, ZW, 0, 128 if t else 136), "z%d" % t)
+        arrive(far(t), R("NL", t), "n%d" % t)
+        arrive(far(t), R("ML", t, ZW, 0, 136), "m%d" % t)
+        arrive(far(t), R("HL", t), "h%d" % t)
+        arrive(home(t), R("BL", t, ZW, 0, 136), "y%d" % t)
+        arrive(far(t), R("VL", t), "v%d" % t)
+        arrive(home(t), R("DL", t, 8), "d%d" % t)
         if t >= 4:
-            arrive(home(t), A("WL", 128 * (t - 4), 128 * (t - 3)), "w%d" % t)
+            arrive(home(t), R("EL", t, 8), "e%d" % t)
 
-    def C(j):
-        return A("col", j, j + 1)
+    def C(j, p=None):
+        return A("col", j, j + 1, p=p)
 
-    PC, PM, PG, P16, WC, CA, CBF, CBN, C1, CN1, WE, TA, TB = range(13)
-    B5, B6, B7 = 5 * 512, 6 * 512, 7 * 512
-    Xw = A("X")
+    PC, PM, PG, P6, P16, WC, WP, WN, CA, CBF, CBN, HI, LO, WE, TA = range(15)
+    B4, B5, B6, B7 = 4 * 512, 5 * 512, 6 * 512, 7 * 512
+    LOW, UPP = slice(0, 64), slice(64, 128)
 
     dma("Y", A("fri"), T.fr0[:], "ld0")
     dma("S", A("pli"), T.pl[:], "ld2")
-    dma("G", A("X", 0, 3072), T.x0[:], "ldx")
-    dma("Y", A("ZS", 128, 256), T.z0[:], "ld1")
+    dma("Y", R("ZS", 0, ZW, 0, 128), T.z0[:], "ld1")
     dma("S", A("b0i"), T.b0[:], "ld3")
-    mset(A("NT"), 0.0)
     iota(A("pint", 0, 4), [[0, 4]], 0, 1, False)
     iota(A("CI", 0, 256), [[1, 256]], 0, 0)
-    mset(A("Zw"), 0.0)
-    mset(A("Zn"), 0.0)
-    mset(A("BASE", 32, 64), 0.0)
-    ts(A("pint", 4, 5), A("pint", 0, 1), 15, ALU.bitwise_and)
-    ts(A("pint", 5, 6), A("pint", 0, 1), 4, ALU.arith_shift_right)
-    ts(A("pint", 8, 12), A("pint", 0, 4), 7, ALU.bitwise_and)
-    copy(C(PC), A("pint", 0, 1))
-    copy(A("col", PM, PG + 1), A("pint", 4, 6))
-    mset(A("BASE", 48, 56), 16.0)
-    ts(A("frb"), A("fri"), -256.0, ALU.add)
-    dma("Y", A("NT", p=slice(0, 128, 16)), A("frb"), "ld4")
-    ts(A("ZS", 256, 264), A("b0i"), -256.0, ALU.add)
-    copy(A("bhu", 0, 8), A("b0i"))
     iota(A("KI", 0, 256), [[1, 16], [0, 16]], 0, 0)
     iota(A("KI", 256, GW), [[1, 16]], 0, 0)
     iota(A("LI", 0, 256), [[0, 16], [1, 16]], 0, 0)
     iota(A("LI", 256, GW), [[0, 16]], -1, 0)
-    send(far(0), A("ZL", 128, 264), A("ZS", 128, 264), "z0")
-    iota(A("X", 3072, XW), [[0, XW - 3072]], 0, 0)
-    iota(A("GI"), [[1, 8], [0, 16]], 0, 0)
+    mset(A("NT"), 0.0)
+    for z_ in ("Zw", "Zn"):
+        mset(A(z_), 0.0)
+    ts(A("pint", 4, 5), A("pint", 0, 1), 15, ALU.bitwise_and)
+    ts(A("pint", 5, 6), A("pint", 0, 1), 4, ALU.arith_shift_right)
+    ts(A("pint", 6, 7), A("pint", 0, 1), 63, ALU.bitwise_and)
+    ts(A("pint", 8, 12), A("pint", 0, 4), 7, ALU.bitwise_and)
+    copy(C(PC), A("pint", 0, 1))
+    copy(A("col", PM, P6 + 1), A("pint", 4, 7))
+    copy(A("off8"), A("pint", 8, 12))
+    ts(A("blk"), A("CI", 0, 8), C(PG), ALU.is_equal)
+    ts(A("Ib"), A("CI", 0, 128), C(PC), ALU.is_equal)
+    ts(A("Zn", 15, 143, 16), A("blk"), 8192.0, ALU.mult)
+    ts(A("Zw", 15, 143, 16), A("blk"), 1.0 / 128, ALU.mult)
+    ts(A("KP"), A("KI"), C(PM), ALU.is_equal, -128.0, ALU.mult)
+    mset(A("KN", 256, GW), 0.0)
+    mset(A("X", 0, SH), 0.0)
+    ts(A("KN", 0, 256), A("KI", 0, 256), C(PM), ALU.is_equal, -128.0, ALU.mult)
+    ts(A("frb"), A("fri"), -256.0, ALU.add)
+    dma("Y", A("NT", SH, E0, p=slice(0, 128, 16)), A("frb"), "ld4")
+    dma("Y", A("X", SH, E0), T.x0[:], "ldx")
+    ts(R("ZS", 0, ZW, 128, 136), A("b0i"), -256.0, ALU.add)
+    send(far(0), R("ZL", 0, ZW, 0, 136), R("ZS", 0, ZW, 0, 136), "z0")
+    ts(A("LP"), A("LI"), C(PM), ALU.is_equal, -128.0, ALU.mult)
+    for s4 in range(4):
+        ts(A("plu", 128 * s4, 128 * s4 + 128), A("pli", s4, 512, 4), float(SH), ALU.add)
+    act(A("NIb"), A("Ib"), ACT.Identity, 0.0, -1.0)
+    for k in range(16):
+        act(A("EXP", k, 2048, 16), A("Ib"), ACT.Copy)
+    mm(P(B7, B7 + 128), R("ZS", 0, ZW, 0, 128), A("Ib"), True, True)
+    act(A("zT"), P(B7, B7 + 128), ACT.Copy)
+    for gg in range(6):
+        act(A("SN", GW * gg, GW * gg + GW), A("KN"), ACT.Identity, 0.0, A("blk", gg, gg + 1))
     iota(A("CI", 256, GW), [[-16, 16]], -2048, 0)
-    iota(A("G8"), [[0, 8], [1, 8]], 0, 0)
-    iota(A("W8"), [[-16, 8], [0, 8]], 257, 0)
-    iota(A("dum"), [[0, 3], [16, 8]], 4096, 0)
+    iota(A("GI"), [[1, 8], [0, 16]], 0, 0)
+    iota(A("JC"), [[0, 2], [256, 8]], 0, 0)
+    iota(A("iG"), [[16, 8]], 0, 0)
+    iota(A("FT"), [[0, 256]], 1, 0)
+    iota(A("RST"), [[0, 256]], 1, 0)
+    iota(A("RST", 0, 256, 16), [[0, 16]], 0, 0)
+    iota(A("T2", 0, 144), [[0, 144]], 0, 0)
+    iota(A("T2", 144, GW), [[0, 128]], 1, 0)
+    iota(A("BASE"), [[0, 56]], 0, 0)
+    iota(A("AT", 40, 48), [[0, 8]], 0, 0)
     for e in range(16):
         iota(A("wrow", e, e + 1), [[0, 1]], WT[e], 0)
+    iota(A("IOT", 0, SH), [[0, SH]], 0, 0)
+    iota(A("IOT", SH, 1024), [[1, 1024 - SH]], 0, 0)
+    ts(A("cnt"), A("pli"), SH - HALF, ALU.add)
+    ts(A("OHW", 0, 256), A("LI", 0, 256), C(PM), ALU.is_equal)
+    ts(A("OHW", 256, 512), A("LI", 0, 256), C(PM), ALU.is_equal)
+    for j in range(1, 8):
+        dma("Y", A("OHW", 512 * j, 512 * j + 512), A("OHW", 0, 512), "ld5")
+    for gg in range(6, 8):
+        ts(A("SN", GW * gg, GW * gg + GW), A("KN"), A("blk", gg, gg + 1), ALU.mult)
+    for gg in range(8):
+        ts(A("SL", GW * gg, GW * gg + GW), A("LP"), A("blk", gg, gg + 1), ALU.mult)
+    ts(C(HI), C(PC), 64.0, ALU.is_ge)
+    ts(C(LO), C(PC), 64.0, ALU.is_lt)
+    ts(C(CA), C(P6), 0.0, ALU.is_equal, 1.0 / 4096, ALU.mult)
+    ts(C(CBF), C(P6), 1.0, ALU.is_equal, 2016.0, ALU.mult)
+    ts(C(CBN), C(P6), 1.0, ALU.is_equal, -2032.0, ALU.mult)
+    ts(C(P16), C(PM), 16.0, ALU.mult)
+    ts(C(WC), C(PC), -1.0, ALU.mult, 256.0, ALU.add)
+    ts(C(WP), C(PC), -BIG, ALU.mult, 256.0 * BIG, ALU.add)
+    ts(C(WN), C(PC), BIG, ALU.mult, -256.0 * BIG, ALU.add)
+    ts(A("blkA", 0, 4), A("blk", 0, 4), C(HI), ALU.add)
+    ts(A("blkA", 4, 8), A("blk", 4, 8), C(LO), ALU.add)
+    mset(A("D1"), -HUGE)
+    mset(A("PRE", 0, 136, 17), -HUGE)
+    for t4 in range(4):
+        iota(A("NDW", GW * t4, GW * t4 + 144), [[0, 144]], 0, 0)
 
-    def expand(dst, src, k0=0, k1=16):
-        for k in range(k0, k1):
-            act(A(dst, k, 2048, 16), src, ACT.Copy)
+    def fold16(buf, lo, cols, out_lo, w):
+        for k in range(16):
+            mm(P(out_lo, out_lo + cols), A(w, 15 - k, 143 - k), A(buf, lo + k, lo + 16 * cols, 16), k == 0, k == 15)
 
-    expand("zxh", A("ZS", 128, 256))
-    for s4 in range(4):
-        copy(A("plu", 128 * s4, 128 * s4 + 128), A("pli", s4, 512, 4))
-    ts(A("LS", 0, 128), A("plu", 0, 128), -2048.0, ALU.add)
-    send(far(0), A("LL", 0, 128), A("LS", 0, 128), "l0")
-    ts(A("blk"), A("CI", 0, 8), C(PG), ALU.is_equal)
-    ts(A("off7"), A("pint", 8, 12), 8.0, ALU.mult, 7.0, ALU.add)
-    copy(A("off8"), A("pint", 8, 12))
-    ts(A("Zw", 15, 143, 16), A("blk"), 1.0 / 128, ALU.mult)
-    ts(A("Zn", 15, 143, 16), A("blk"), 4096.0, ALU.mult)
-    ts(A("cnt"), A("pli"), -HALF, ALU.add)
+    def ccol(t):
+        return A("CN", t % 4, 512, 4)
 
-    def names_chunk(ch, eng):
+    def names(ch, eng):
         src = IND(A("NT"), A("plu", 64 * ch, 64 * ch + 64))
         out = A("NW", 1024 * ch, 1024 * ch + 1024)
         if eng == "S":
@@ -289,332 +330,332 @@ def rank_program(g, core, T, topo):
         else:
             copy(out, src)
 
-    def fold16(buf, lo, cols, out_lo, w="Zw"):
-        for k in range(16):
-            mm(P(out_lo, out_lo + cols), A(w, 15 - k, 143 - k), A(buf, lo + k, lo + 16 * cols, 16), k == 0, k == 15)
-
-    def fold_names(ch):
-        fold16("NW", 1024 * ch, 64, (B6 if ch < 2 else B7) + 64 * ch, "Zn")
-
-    for ch in range(3):
-        names_chunk(ch, "S")
-    for ch in range(2):
-        fold_names(ch)
-    act(A("ZS", 0, 128), P(B6, B6 + 128), ACT.Identity, 0.0, -1.0 / 64)
-    send(far(0), A("ZL", 0, 128), A("ZS", 0, 128), "n0")
-    iota(A("hmin", 2048, 4096), [[0, 2048]], 63, 0)
-    iota(A("IOT", 0, 512), [[1, 512]], 0, 0)
-    for ch in range(3, 7):
-        names_chunk(ch, "S")
-    for ch in range(2, 4):
-        fold_names(ch)
-
-    ts(A("KP"), A("KI"), C(PM), ALU.is_equal, -128.0, ALU.mult)
-    ts(A("LP"), A("LI"), C(PM), ALU.is_equal, -128.0, ALU.mult)
-    ts(A("KN", 256, GW), A("KI", 256, GW), 0.0, ALU.mult)
-    copy(A("KN", 0, 256), A("KP", 0, 256))
-    for gg in range(8):
-        ts(A("SK", GW * gg, GW * gg + GW), A("KP"), A("blk", gg, gg + 1), ALU.mult)
-        ts(A("SL", GW * gg, GW * gg + GW), A("LP"), A("blk", gg, gg + 1), ALU.mult)
-        ts(A("SN", GW * gg, GW * gg + GW), A("KN"), A("blk", gg, gg + 1), ALU.mult)
-    ts(C(P16), C(PM), 16.0, ALU.mult)
-    ts(C(WC), C(PC), -1.0, ALU.mult, 256.0, ALU.add)
-    ts(C(CA), C(PC), 0.0, ALU.is_equal, 1.0 / 4096, ALU.mult)
-    ts(C(C1), C(PC), 1.0, ALU.is_equal)
-    ts(C(CN1), C(PC), 1.0, ALU.not_equal)
-    ts(C(TA), C(PC), 2.0, ALU.is_equal, 2016.0, ALU.mult)
-    ts(C(TB), C(PC), 2.0, ALU.is_equal, -2017.0, ALU.mult)
-    ts(A("BLK"), A("GI"), C(PG), ALU.is_equal)
-    ts(A("Ib"), A("CI", 0, 128), C(PC), ALU.is_equal)
-    ts(C(CBF), C(C1), 1.0 / 16, ALU.mult, C(TA), ALU.add)
-    ts(C(CBN), C(C1), -1.0 / 16, ALU.mult, C(TB), ALU.add)
-    ts(A("CL"), A("GI"), C(C1), ALU.mult, C(CN1), ALU.add)
-    ts(A("I17"), A("CI", 0, 32), C(PM), ALU.is_equal)
-    ts(A("T1"), A("CI", 0, 32), 16.0, ALU.is_lt)
-    ts(A("BS8"), A("blk"), 4096.0, ALU.mult)
-    ts(A("CR", 0, 256), A("CI", 0, 256), C(CA), ALU.mult, C(CBF), ALU.add)
-    ts(A("CR", 256, GW), A("CI", 256, GW), C(CA), ALU.mult, C(CBN), ALU.add)
-    ts(A("TR", 0, 128), A("CI", 0, 128), C(PC), ALU.is_lt, 0.5, ALU.mult)
-    ts(A("sc", 0, 128), A("LI", 0, 128), C(PM), ALU.is_equal, 133120.0, ALU.mult)
-    copy(A("CR", GW, 2 * GW), A("CR", 0, GW))
-    copy(A("CR", 2 * GW, 3 * GW), A("CR", 0, GW))
-    ts(A("RST"), A("LI", 0, 256), 0.0, ALU.not_equal)
-    ts(A("RS8"), A("G8"), 0.0, ALU.not_equal)
-    ts(A("wt2"), A("G8"), C(PG), ALU.is_equal)
-    ts(A("W8"), A("W8"), C(PM), ALU.subtract)
-    ts(A("dum"), A("dum"), C(PM), ALU.add)
-    tt(A("wtmp"), A("wrow"), A("I17", 0, 16), ALU.mult)
-    tt(A("wt2"), A("wt2"), A("W8"), ALU.mult)
-    copy(A("BASE", 16, 32), A("dum", 0, 16))
-    red(C(WE), A("wtmp"), ALU.add, False)
-    ts(A("WT64"), A("wt2"), -1.0, ALU.add)
-    ts(A("WB"), A("BLK"), C(WE), ALU.mult)
+    def table_constants():
+        act(A("CR", 0, 256), A("CI", 0, 256), ACT.Identity, C(CBF), C(CA))
+        act(A("CR", 256, GW), A("CI", 256, GW), ACT.Identity, C(CBN), C(CA))
 
     def late_constants():
+        act(A("KA", p=LOW), A("KP", p=LOW), ACT.Copy)
+        act(A("KB", p=UPP), A("KP", p=UPP), ACT.Copy)
+        act(A("KA", p=UPP), A("CR", p=UPP), ACT.Copy)
+        act(A("KB", p=LOW), A("CR", p=LOW), ACT.Copy)
         for gg in range(8):
-            act(A("SG", 128 * gg, 128 * gg + 128), A("BLK"), ACT.Identity, A("blk", gg, gg + 1), 0.0)
-        act(A("blkb"), A("blk"), ACT.Copy)
-        for j in range(2):
-            act(A("MD", 128 * j, 128 * j + 128), A("sc", 0, 128), ACT.Identity, -131072.0, 1.0)
+            act(A("SK", GW * gg, GW * gg + GW), A("KA" if gg < 4 else "KB"), ACT.Identity, 0.0, A("blkA", gg, gg + 1))
+        ts(A("I16"), A("CI", 0, 16), C(PM), ALU.is_equal)
+        ts(A("BS8"), A("blk"), 4096.0, ALU.mult)
+        ts(A("TR", 0, 128), A("CI", 0, 128), C(PC), ALU.is_lt, 0.5, ALU.mult)
+        ts(A("iG"), A("iG"), C(PM), ALU.add)
+        ts(A("BLK"), A("GI"), C(PG), ALU.is_equal)
+        tt(A("wtmp"), A("wrow"), A("I16"), ALU.mult)
+        ts(A("JC"), A("JC"), C(P16), ALU.add)
+        ts(A("G48", 0, 8), A("iG"), BIG, ALU.mult, 8192.0 - 256 * BIG - HUGE, ALU.add)
+        ts(A("G48", 8, 16), A("iG"), -BIG, ALU.mult, 8192.0 + 256 * BIG - HUGE, ALU.add)
+        red(C(WE), A("wtmp"), ALU.add, False)
+        act(A("I128"), A("Ib"), ACT.Identity, 0.0, 128.0)
+        act(A("CIb"), A("CI", 0, 128), ACT.Copy)
         for j in range(1, 4):
             act(A("TR", 128 * j, 128 * j + 128), A("TR", 0, 128), ACT.Copy)
-        act(A("NIb"), A("Ib"), ACT.Identity, 0.0, -1.0)
         act(A("I32"), A("Ib"), ACT.Copy)
-        act(A("NI32"), A("Ib"), ACT.Identity, 0.0, -1.0)
-        act(A("ymin", 2048, 4096), A("hmin", 2048, 4096), ACT.Copy)
+        act(A("MD"), A("OHW", 0, 256), ACT.Identity, -131072.0, 131072.0 + MID)
+        act(A("blkb"), A("blk"), ACT.Copy)
+        for gg in range(8):
+            for h in range(2):
+                act(A("PRE", 1 + 8 * h + gg, 136, 17), A("G48", 8 * h, 8 * h + 8), ACT.Identity, HUGE, A("blk", gg, gg + 1))
+        for gg in range(8):
+            act(A("SG", 128 * gg, 128 * gg + 128), A("Ib"), ACT.Identity, A("blk", gg, gg + 1), 0.0)
+        act(A("WB"), A("BLK"), ACT.Identity, 0.0, C(WE))
+        for o in (24, 40, 48):
+            act(A("BASE", o, o + 8), A("iG"), ACT.Copy)
+        act(A("D1", 16, 136, 17), A("iG"), ACT.Copy)
+        act(A("AT", 32, 40), A("iG"), ACT.Identity, 144.0, 1.0)
+        for t4 in range(4):
+            act(A("FIN", 72 * t4 + 8, 72 * t4 + 16), A("iG"), ACT.Identity, 16.0, 1.0)
 
     banks = [(0, 512), (512, 1024), (1024, 1536), (1536, 2048), (2048, SW)]
 
-    def spass(lhsT, sel, start, stop, which=banks):
-        for lo, hi in which:
+    def spass(lhsT, sel, start, stop, which):
+        for b in which:
+            lo, hi = banks[b]
             mm(P(lo, hi), lhsT, A(sel, lo, hi), start, stop)
 
-    def ccol(t):
-        return A("CN", t % 4, 512, 4)
+    def kpass(b):
+        lo, hi = banks[b]
+        cut = 4 * GW
+        for a_, b_, j in ((lo, min(hi, cut), 0), (max(lo, cut), hi, 1)):
+            if a_ < b_:
+                mm(P(a_, b_), A("FT", 128 * j, 128 * j + 128), A("SK", a_, b_), False, False)
 
     def lnames(t):
-        act(A("Lr"), ccol(t), ACT.Identity, ROUND, 1.0 / 4096)
-        act(A("ZS", ZW * t, ZW * t + 128), A("Lr"), ACT.Identity, 64.0 * ROUND, -64.0)
+        act(A("Lr"), ccol(t), ACT.Identity, ROUND, 1.0 / 8192)
+        act(A("NH"), A("Lr"), ACT.Identity, 64.0 * ROUND, -64.0)
 
     def lprep(t):
         ts(A("Li"), ccol(t), HALF, ALU.add)
-        ts(A("La"), A("Li"), 4095, ALU.bitwise_and)
-        copy(A("Lu"), A("La"))
-        ts(A("LS", 128 * t, 128 * t + 128), A("Lu"), -2048.0, ALU.add)
-        send(far(t), A("LL", 256 * t, 256 * t + 128), A("LS", 128 * t, 128 * t + 128), "l%d" % t)
-
-    def lists(t):
-        q0 = 80 * t
-        d = A("dlt", 128 * t, 128 * t + 128) if t < 4 else A("dl2")
-        reg = P(B7 + 256, B7 + 384)
-        mm(reg, A("I32"), ccol(t), True, False)
-        tt(d, IND(A("I17"), A("QL", q0 + 48, q0 + 56)), A("nd"), ALU.mult)
-        if t >= 4:
-            tt(A("tc"), IND(A("IOT", 0, 16), A("QL", q0 + 64, q0 + 72)), A("dlt", 128 * (t - 4), 128 * (t - 3)), ALU.mult)
-        mm(reg, A("I32"), d, False, t < 4)
-        if t >= 4:
-            mm(reg, A("NI32"), A("tc"), False, True)
-        act(ccol(t), reg, ACT.Copy)
-
-    def entries(t):
-        tt(A("X", 3072 + 128 * t, 3200 + 128 * t), IND(A("T1"), A("QL", 80 * t + 48, 80 * t + 56)),
-           A("VS", 128 * t, 128 * t + 128), ALU.mult)
-
-    def records(t):
-        q0 = 80 * t
-        for j, o in ((0, 56), (1, 32), (2, 40)):
-            act(A("REC", 1024 * j + 128 * t, 1024 * j + 128 * t + 128), IND(A("IOT"), A("QL", q0 + o, q0 + o + 8)), ACT.Copy)
+        ts(A("La"), A("Li"), 8191, ALU.bitwise_and)
+        copy(R("Lu", t % 2), A("La"))
+        ts(R("L16", t % 2), R("Lu", t % 2), -float(MID), ALU.add)
 
     def mprep(t):
         ts(A("Mi"), IND(A("CN"), A("bfu")), HALF, ALU.add)
-        act(A("Mr"), IND(A("CN"), A("bfu")), ACT.Identity, ROUND, 1.0 / 4096)
-        act(A("NM"), A("Mr"), ACT.Identity, -64.0 * ROUND, 64.0)
-        ts(A("Ma"), A("Mi"), 4095, ALU.bitwise_and)
+        mnames(t)
+        ts(A("Ma"), A("Mi"), 8191, ALU.bitwise_and)
         copy(A("Mu"), A("Ma"))
+        ts(R("MS", t, ZW, 0, 128), A("Mu"), -float(MID), ALU.add)
+        send(home(t), R("ML", t, ZW, 0, 136), R("MS", t, ZW, 0, 136), "m%d" % t)
 
-    def gmin(out, offs, zx, h, wide):
-        tt(A(out, 1024 * h, 1024 * h + 1024), IND(A("X", 0, wide), A(offs, 64 * h, 64 * h + 64)),
-           A(zx, 1024 * h, 1024 * h + 1024), ALU.min)
+    def mnames(t):
+        act(A("Mr"), IND(A("CN"), A("bfu")), ACT.Identity, ROUND, 1.0 / 8192)
+        act(R("NS", t), A("Mr"), ACT.Identity, -64.0 * ROUND, 64.0)
+        send(home(t), R("NL", t), R("NS", t), "n%d" % t)
+
+    def expand(t, k0=0, k1=16):
+        for k in range(k0, k1):
+            act(A("zxf", k, 2048, 16), R("ZL", t, ZW, 0, 128), ACT.Copy)
+
+    def codec(s4):
+        ts(A("fri", 0, 128), ccol(s4), HALF, ALU.add)
+        ts(A("pli", 0, 128), A("fri", 0, 128), 8191, ALU.bitwise_and)
+        ts(A("cnt", s4, 512, 4), A("pli", 0, 128), -float(SH), ALU.add)
+
+    def records(t):
+        for j, o in ((0, 16), (1, 0), (2, 8)):
+            act(A("REC", 1024 * j + 128 * t, 1024 * j + 128 * t + 128), IND(A("IOT"), R("Q", t, 56, o, o + 8)), ACT.Copy)
+
+    def blockx(t):
+        return A("X", E0 + 128 * t, E0 + 128 * t + 128)
+
+    def mask(t):
+        tt(blockx(t), IND(A("T2"), R("Q", t, 56, 32, 40)), blockx(t), ALU.mult)
+
+    def zpart(c):
+        b = B5 + 512 * (c % 2)
+        mm(P(b, b + 512), A("zT"), A("EXP", 512 * c, 512 * c + 512), True, True)
+
+    def ygather(t, c):
+        yw = E0 + 128 * max(0, t - 3)
+        act(A("ybuf", 1024 * c, 1024 * c + 1024), IND(A("X", 0, yw), R("Lu", t % 2, 128, 64 * c, 64 * c + 64)), ACT.Copy)
+
+    def ymin(c):
+        b = B5 + 512 * (c % 2)
+        tt(A("rbuf", 512 * c, 512 * c + 512), A("ybuf", 512 * c, 512 * c + 512), P(b, b + 512), ALU.min)
+
+    def emrows(gg):
+        return (T.EM[:, gg:64:8, :], [("EM", gg, gg + 1, 1)])
+
+    for ch, eng in enumerate("VSVSVVSV"):
+        names(ch, eng)
+        if ch == 3:
+            expand(0)
+            ts(A("bfu"), R("ZL", 0, ZW, 128, 136), 256.0, ALU.add)
+            ts(A("Mu"), IND(A("pli"), A("bfu")), float(SH), ALU.add)
+            copy(R("MS", 0, ZW, 128, 136), A("bfu"))
+            ts(R("MS", 0, ZW, 0, 128), A("Mu"), -float(MID), ALU.add)
+            send(home(0), R("ML", 0, ZW, 0, 136), R("MS", 0, ZW, 0, 136), "m0")
+            copy(R("Lu", 0), A("plu", 0, 128))
+            ts(R("L16", 0), A("plu", 0, 128), -float(MID), ALU.add)
+        if ch % 2:
+            s4 = ch // 2
+            fold16("NW", 2048 * s4, 128, 512 * s4, "Zn")
+    zpart(0)
+    zpart(1)
+    for s4 in range(4):
+        tt(ccol(s4), P(512 * s4, 512 * s4 + 128), A("cnt", s4, 512, 4), ALU.add)
+    mnames(0)
+    lnames(0)
+    spass(A("NH"), "SN", True, False, range(5))
+    table_constants()
 
     for t in range(NR):
-        yw = 3072 + 128 * max(0, t - 3)
-        z0_, l0, d0, q0 = ZW * t, 256 * t, 144 * t, 80 * t
-        vs = A("VS", 128 * t, 128 * t + 128)
-        vl = A("VL", 128 * t, 128 * t + 128)
-        zl = A("ZL", z0_ + 128, z0_ + 256)
-        bl = A("ZL", z0_ + 256, z0_ + 264)
-        fs, fl = A("FS", 128 * t, 128 * t + 128), A("FL", 128 * t, 128 * t + 128)
-        if t > 0:
-            lists(t - 1)
-            spass(A("ZL", z0_, z0_ + 128), "SN", True, False)
-            gmin("ymin", "Lu", "zxh", 0, yw)
-            fold16("ymin", 0, 64, B5)
-            ts(A("bfu"), bl, 256.0, ALU.add)
-            mprep(t)
-            expand("zxf", zl)
-            spass(A("NM"), "SL", False, False)
-            gmin("ymin", "Lu", "zxh", 1, yw)
-            fold16("ymin", 1024, 64, B5 + 64)
-            entries(t - 1)
-            ts(A("LL", l0 + 128, l0 + 256), A("Mu"), -2048.0, ALU.add)
-            copy(fs, P(B5, B5 + 128))
-            send(far(t), fl, fs, "f%d" % t)
-            records(t - 1)
-        else:
-            for h in range(2):
-                gmin("ymin", "plu", "zxh", h, yw)
-                fold16("ymin", 1024 * h, 64, B5 + 64 * h)
-                fold_names(4 + h)
-            ts(A("bfu"), bl, 256.0, ALU.add)
-            names_chunk(7, "V")
-            copy(fs, P(B5, B5 + 128))
-            send(far(t), fl, fs, "f%d" % t)
-            expand("zxf", zl)
-            for ch in (6, 7):
-                fold_names(ch)
-            spass(A("ZL", 0, 128), "SN", True, False)
-            for s4 in range(4):
-                lo = (B6 if s4 == 0 else B7) + 128 * s4
-                tt(ccol(s4), P(lo, lo + 128), A("cnt", s4, 512, 4), ALU.add)
-            mprep(0)
-            ts(A("LL", l0 + 128, l0 + 256), A("Mu"), -2048.0, ALU.add)
-            late_constants()
-            iota(A("IOT", 512, 4096), [[1, 3584]], 512, 0)
-            spass(A("NM"), "SL", False, False)
-        act(A("nv"), IND(A("IOT", 0, 512), A("bhu", 8 * t, 8 * t + 8)), ACT.Identity, -256.0 * 4096 - HALF, 4096.0)
-        if t >= 4:
-            ws, wl = A("WS", 128 * (t - 4), 128 * (t - 3)), A("WL", 128 * (t - 4), 128 * (t - 3))
-            act(ws, A("X", 3072 + 128 * (t - 4), 3072 + 128 * (t - 3)), ACT.Copy)
-            send(far(t), wl, ws, "w%d" % t)
-            act(A("c63"), ws, ACT.Identity, 63.0, -1.0)
-        if t < NR - 1:
-            lnames(t + 1)
-        if t >= 4:
-            act(A("f63"), wl, ACT.Identity, 63.0, -1.0)
-        for lo, hi in banks:
-            mm(P(lo, hi), A("CL", p=slice(0, 3)), A("CR", lo % GW, lo % GW + hi - lo, p=slice(0, 3)), False, False)
+        xw = A("X", 0, E0 + 128 * t)
+        last = t == NR - 1
         for h in range(2):
-            gmin("hmin", "Mu", "zxf", h, XW)
-            if h == 1:
-                spass(fl, "SK", False, False, banks[0:2])
-            fold16("hmin", 1024 * h, 64, B6 + 64 * h)
-        spass(fl, "SK", False, False, banks[2:3])
-        copy(A("HS"), P(B6, B6 + 128))
-        spass(A("HS"), "SL", False, True, banks[0:3])
-        for b in (3, 4):
-            spass(fl, "SK", False, False, banks[b:b + 1])
-            spass(A("HS"), "SL", False, True, banks[b:b + 1])
+            tt(A("hmin", 1024 * h, 1024 * h + 1024), IND(xw, A("Mu", 64 * h, 64 * h + 64)), A("zxf", 1024 * h, 1024 * h + 1024), ALU.min)
+        for c in range(2):
+            ygather(t, c)
+        if t > 0:
+            spass(R("NL", t), "SL", False, False, range(5))
+        fold16("hmin", 0, 64, B7, "Zw")
+        fold16("hmin", 1024, 64, B7 + 64, "Zw")
+        ymin(0)
+        ymin(1)
+        zpart(2)
+        zpart(3)
+        copy(R("HS", t), P(B7, B7 + 128))
+        send(home(t), R("HL", t), R("HS", t), "h%d" % t)
+        ymin(2)
+        ymin(3)
+        fold16("rbuf", 0, 64, B7 + 128, "Zw")
+        fold16("rbuf", 1024, 64, B7 + 192, "Zw")
+        if t == 0:
+            spass(R("NL", t), "SL", False, False, range(5))
+            late_constants()
+            iota(A("hmin", 2048, 4096), [[0, 2048]], 63, 0)
+        else:
+            mask(t - 1)
+            records(t - 1)
+        ts(A("AT", 16, 24), R("ML", t, ZW, 128, 136), float(SH), ALU.add)
+        copy(A("bu"), R("ML", t, ZW, 128, 136))
+        if not last:
+            lprep(t + 1)
+        if t > 4:
+            codec(t - 5)
+        copy(A("FT", 0, 128, p=LOW), P(B7 + 128, B7 + 256, p=LOW))
+        copy(A("FT", 128, 256, p=UPP), P(B7 + 128, B7 + 256, p=UPP))
+        for b in range(5):
+            kpass(b)
+            spass(R("HL", t), "SL", False, True, (b,))
+        ndw = GW * (t % 4)
+        act(A("nv"), IND(A("IOT", SH, SH + 512), A("bu")), ACT.Identity, -256.0 * 64, 64.0)
+        reg = P(B6 + 256, B6 + 384)
+        mm(reg, A("I128"), A("NH"), True, False)
+        mm(reg, A("Ib"), A("CIb"), False, False)
+        mm(reg, A("NIb"), R("L16", t % 2), False, False)
+        mm(reg, A("I128"), A("nv"), False, True)
         for gg in range(8):
             red(A("U", gg, gg + 1), P(GW * gg, GW * gg + GW), ALU.min, True)
             if gg < 7:
-                act(A("UX", 16 * gg, 16 * gg + 16), A("I17", 0, 16), ACT.Identity, 0.0, A("U", gg, gg + 1))
-        ts(A("UX", 112, 128), A("I17", 0, 16), A("U", 7, 8), ALU.mult)
-        mm(P(B6, B6 + 256), A("Ib"), A("MD"), True, False)
-        for b in range(3):
-            mm(P(512 * b, 512 * b + 512), A("Ib"), A("TR"), True, False)
+                act(A("UX", 16 * gg, 16 * gg + 16), A("I16"), ACT.Identity, 0.0, A("U", gg, gg + 1))
+            if gg == 4:
+                act(A("NDW", ndw + 144, ndw + GW), reg, ACT.Identity, float(E0 + 128 * t - MID), 1.0)
+        mm(P(0, 512), A("Ib"), A("TR"), True, False)
+        ts(A("UX", 112, 128), A("I16"), A("U", 7, 8), ALU.mult)
         mm(P(B5, B5 + 8), A("UX"), A("BS8"), True, True)
-        for b in (3, 4):
-            mm(P(512 * b, 512 * b + 256), A("Ib"), A("TR", 0, 256), True, False)
+        for b in (512, 1024, 1536):
+            mm(P(b, b + 512), A("Ib"), A("TR"), True, False)
+        mm(P(B7 + 256, B7 + 512), A("Ib"), A("MD"), True, False)
+        mm(P(B4, B4 + 136), A("I32"), A("PRE"), True, False)
         ts(A("r1"), A("U"), 2017.0, ALU.is_lt, C(WC), ALU.mult)
-        ts(A("V6", 40, 48), bl, 256.0, ALU.add)
         copy(A("Ui"), P(B5, B5 + 8))
-        ts(A("dec", 16, 24), A("Ui"), 0xF0F, ALU.bitwise_and)
-        ts(A("dec", 0, 8), A("Ui"), 4, ALU.logical_shift_right, 15, ALU.bitwise_and)
-        ts(A("dec", 24, 32), A("Ui"), 0xF00, ALU.bitwise_and)
-        ts(A("offH"), A("dec", 16, 24), C(P16), ALU.add)
-        ts(A("dec", 8, 16), A("Ui"), 15, ALU.bitwise_and)
-        tt(A("ok"), A("dec", 24, 32), A("dec", 0, 8), ALU.add)
-        copy(A("klu"), A("dec", 0, 16))
-        ts(A("DS", d0 + 128, d0 + 136), A("ok"), C(P16), ALU.add)
-        act(A("DS", d0, d0 + 128), IND(A("hmin"), A("offH")), ACT.Copy)
-        send(home(t), A("DL", d0, d0 + 136), A("DS", d0, d0 + 136), "d%d" % t)
-        tt(A("LM"), IND(A("I17"), A("klu")), A("LL", l0, l0 + 256), ALU.mult)
-        for j in range(2):
-            mm(P(B5 + 64 + 8 * j, B5 + 72 + 8 * j), A("LM", 128 * j, 128 * j + 128), A("blkb"), True, True)
-
-        def dpos(j, gg):
-            return 128 * gg if j == 0 else 1024 + 128 * gg + (256 if gg >= 6 else 0)
-
-        def spread(j, g0, g1):
-            for gg in range(g0, g1):
-                mm(P(dpos(j, gg), dpos(j, gg) + 128), A("SG", 128 * gg, 128 * gg + 128), A("LM", 128 * j, 128 * j + 128),
-                   False, gg == g1 - 1)
-
-        def emrows(gg):
-            return (T.EM[:, gg:64:8, :], [("EM", gg, gg + 1, 1)])
-
-        mm(P(B6, B6 + 256), A("BLK"), A("LM"), False, True)
-        spread(1, 0, 4)
-        spread(0, 0, 4)
-        spread(0, 4, 8)
-        spread(1, 4, 6)
-        spread(1, 6, 8)
-        copy(A("V6", 32, 40), A("dec", 0, 8))
-        if t >= 4:
-            ts(A("nf"), A("Ui"), 2017.0 * 4096, ALU.is_ge)
-        copy(A("cm"), P(B5 + 64, B5 + 80))
-        scan(A("sc"), A("RST"), P(B6, B6 + 256), ALU.max)
-        copy(A("CS", 16 * t, 16 * t + 16), A("sc", 15, 256, 16))
-        if t < NR - 1:
-            send(home(t), A("CD", 8 * t, 8 * t + 8), A("CS", 16 * t, 16 * t + 8), "c%d" % t)
-        for g0, g1 in ((0, 4), (4, 6)):
-            for gg in range(g0, g1):
-                act(A("AB", 128 * gg, 128 * gg + 128), P(dpos(1, gg), dpos(1, gg) + 128), ACT.Abs, A("cm", 8 + gg, 9 + gg), -1.0)
-            for gg in range(g0, g1):
+        ts(A("dec", 8, 16), A("Ui"), 4, ALU.logical_shift_right, 15, ALU.bitwise_and)
+        ts(A("dec", 0, 8), A("Ui"), 0x80F, ALU.bitwise_and)
+        tt(R("BS", t, ZW, 128, 144), A("dec"), A("JC"), ALU.add)
+        copy(A("OF"), R("BS", t, ZW, 128, 144))
+        oy, ol = A("OF", 8, 16), A("OF", 0, 8)
+        act(R("BS", t, ZW, 0, 128), IND(A("ybuf"), oy), ACT.Copy)
+        send(far(t), R("BL", t, ZW, 0, 136), R("BS", t, ZW, 0, 136), "y%d" % t)
+        lc, lm = A("LM", 0, 128), A("LM", 128, 256)
+        tt(lc, IND(A("OHW"), oy), R("L16", t % 2), ALU.mult)
+        tt(lm, IND(A("OHW"), ol), R("ML", t, ZW, 0, 128), ALU.mult)
+        if not last:
+            act(A("ykb"), R("BS", t, ZW, 0, 128), ACT.Copy)
+            mm(P(B6, B6 + 128), A("NIb"), R("ZS", t, ZW, 0, 128), True, False)
+        mm(P(B5 + 16, B5 + 24), lc, A("blkb"), True, True)
+        if not last:
+            mm(P(B6, B6 + 128), A("Ib"), A("ykb"), False, True)
+        mm(P(B5 + 24, B5 + 32), lm, A("blkb"), True, True)
+        for gg in range(8):
+            mm(P(256 * gg, 256 * gg + 256), A("SG", 128 * gg, 128 * gg + 128), A("LM"), False, gg % 2 == 1)
+        mm(P(B7 + 256, B7 + 512), A("BLK"), A("LM"), False, True)
+        copy(A("cm"), P(B5 + 16, B5 + 32))
+        if not last:
+            act(R("ZS", t + 1, ZW, 0, 128), P(B6, B6 + 128), ACT.Abs)
+            send(far(t + 1), R("ZL", t + 1, ZW, 0, 128), R("ZS", t + 1, ZW, 0, 128), "z%d" % (t + 1))
+        for gg in range(8):
+            ts(A("EC", 128 * gg, 128 * gg + 128), P(256 * gg, 256 * gg + 128), A("cm", gg, gg + 1), ALU.is_equal)
+        for g0 in (0, 2):
+            for gg in (g0, g0 + 1):
+                act(A("AB", 128 * gg, 128 * gg + 128), P(256 * gg + 128, 256 * gg + 256), ACT.Abs, A("cm", 8 + gg, 9 + gg), -1.0)
+            for gg in (g0, g0 + 1):
                 act(emrows(gg), A("AB", 128 * gg, 128 * gg + 128), ACT.Relu, 1.0, -2.0)
         for gg in range(8):
-            ts(A("EC", 128 * gg, 128 * gg + 128), P(128 * gg, 128 * gg + 128), A("cm", gg, gg + 1), ALU.is_equal)
-            mm(P(B7 + gg, B7 + gg + 1), A("EC", 128 * gg, 128 * gg + 128), A("r1", gg, gg + 1), True, True)
+            mm(P(B5 + 32 + gg, B5 + 33 + gg), A("EC", 128 * gg, 128 * gg + 128), A("r1", gg, gg + 1), True, True)
+        scan(A("sc"), A("RST"), P(B7 + 256, B7 + 512), ALU.mult, ALU.max)
         for gg in (6, 7):
-            ts(emrows(gg), P(dpos(1, gg), dpos(1, gg) + 128), A("cm", 8 + gg, 9 + gg), ALU.is_equal)
-        ts(A("r2"), P(B7, B7 + 8), C(WC), ALU.is_equal, C(WC), ALU.mult)
-        for c in range(8):
-            mm(P(B5 + 8 * c, B5 + 8 * c + 8), (T.EM[:, 8 * c:8 * c + 8, :], [("EM", 0, 8, 1)]), A("r2"), True, True)
-        act(A("V6", 0, 16), A("sc", 15, 256, 16), ACT.Copy)
-        act(A("V6", 16, 32), A("sc", 15, 256, 16), ACT.Copy)
-        act(A("Bm"), IND(Xw, A("CS", 16 * t + 8, 16 * t + 16)), ACT.Copy)
+            ts(emrows(gg), P(256 * gg + 128, 256 * gg + 256), A("cm", 8 + gg, 9 + gg), ALU.is_equal)
+        ts(A("r2", 0, 8), P(B5 + 32, B5 + 40), C(WC), ALU.is_equal, C(WP), ALU.mult)
+        ts(A("r2", 8, 16), P(B5 + 32, B5 + 40), C(WC), ALU.is_equal, C(WN), ALU.mult)
+        for gg in (4, 5):
+            ts(emrows(gg), P(256 * gg + 128, 256 * gg + 256), A("cm", 8 + gg, 9 + gg), ALU.is_equal)
+        cg, mg = A("sc", 15, 128, 16), A("sc", 143, 256, 16)
+        act(A("D1", 0, 136, 17), mg, ACT.Copy)
+        act(A("AT", 0, 16), A("sc", 15, 256, 16), ACT.Copy)
+        act(A("AT", 24, 32), cg, ACT.Copy)
         if t >= 4:
-            p0 = 48 * (t - 4)
-            ts(A("ge"), A("sc", 15, 128, 16), 3072.0, ALU.is_ge)
-            tt(A("DM", p0 + 16, p0 + 24), A("sc", 15, 128, 16), A("dum", 0, 8), ALU.subtract)
-            tt(A("cls"), A("nf"), A("ge"), ALU.mult)
-            tt(A("t3"), IND(A("cls"), A("off8", 0, 2)), A("DM", p0, p0 + 32), ALU.mult)
-            copy(A("QS", q0 + 64, q0 + 72), A("cls"))
-            tt(A("BASE", 0, 24), A("t3", 0, 24), A("dum"), ALU.add)
-            copy(A("QS", q0, q0 + 16), A("BASE", 0, 16))
-        tt(A("DM", 48 * t, 48 * t + 48), A("V6"), A("BASE", 16, 64), ALU.subtract)
-        copy(A("cu"), A("DL", d0 + 128, d0 + 136))
-        tt(A("E64"), P(B5, B5 + 64), A("WT64"), ALU.is_equal)
-        tt(vs, IND(A("ymin"), A("cu")), A("DL", d0, d0 + 128), ALU.min)
-        send(far(t), vl, vs, "v%d" % t)
-        scan(A("B64"), A("RS8"), A("E64"), ALU.add)
-        tt(A("G48"), IND(A("B64"), A("off7", 0, 3)), A("DM", 48 * t, 48 * t + 48), ALU.mult)
-        tt(A("FIN"), A("G48"), A("BASE", 16, 64), ALU.add)
-        copy(A("QS", q0 + 16, q0 + 64), A("FIN"))
-        send(home(t), qpart("QL", t), qpart("QS", t), "q%d" % t)
-        if t < NR - 1:
-            z1 = z0_ + ZW
-            act(A("yk"), IND(Xw, A("CD", 8 * t, 8 * t + 8)), ACT.Copy)
-            reg = P(B7 + 384, B7 + 512)
-            mm(reg, A("NIb"), A("ZS", z0_ + 128, z0_ + 256), True, False)
-            mm(reg, A("Ib"), A("yk"), False, True)
-            act(A("ZS", z1 + 128, z1 + 256), reg, ACT.Abs)
-            mm(P(B6, B6 + 128), A("Ib"), A("MD", 0, 128), True, False)
-            mm(P(B6, B6 + 128), A("WB"), A("ZS", z1 + 128, z1 + 256), False, True)
-            lprep(t + 1)
-            scan(A("su"), A("RST", 0, 128), P(B6, B6 + 128), ALU.max)
-            copy(A("ui"), A("su", 15, 128, 16))
-            ts(A("ub"), A("ui"), 511, ALU.bitwise_and)
-            ts(A("ZS", z1 + 256, z1 + 264), A("ub"), -256.0, ALU.add)
-            send(far(t + 1), A("ZL", z1, z1 + 264), A("ZS", z1, z1 + 264), "z%d" % (t + 1))
-            copy(A("bhu", 8 * t + 8, 8 * t + 16), A("ub"))
-        reg = P(B7 + 128, B7 + 256)
-        mm(reg, A("I32"), A("nv"), True, False)
-        mm(reg, A("I32"), A("IOT", 3072 + 128 * t, 3200 + 128 * t), False, False)
-        mm(reg, A("NI32"), ccol(t), False, True)
-        if t < NR - 1:
-            expand("zxh", A("ZS", z1 + 128, z1 + 256))
-        act(A("nd"), reg, ACT.Copy)
-        tt(IND(Xw, A("QS", q0 + 24, q0 + 32)), A("Bm"), vl, ALU.subtract)
-        oc = A("QL", q0 + 16, q0 + 24)
-        tt(A("tk"), IND(Xw, oc), vs, ALU.max)
-        tt(IND(Xw, oc), A("tk"), vs, ALU.subtract)
+            act(R("FIN", t - 4, 72, 0, 8), cg, ACT.Copy)
+        for j in range(8):
+            mm(P(B4 + 17 * j + 1, B4 + 17 * j + 17), (T.EM[:, 8 * j:8 * j + 8, :], [("EM", 0, 8, 1)]), A("r2"), False, j == 7)
         if t >= 4:
-            for off, cap, w in ((A("QL", q0, q0 + 8), A("c63"), ws), (A("QS", q0 + 8, q0 + 16), A("f63"), wl)):
-                tt(A("tk"), IND(Xw, off), cap, ALU.min)
-                tt(IND(Xw, off), A("tk"), w, ALU.add)
+            ts(A("nfb"), R("BS", t, ZW, 128, 136), 2048.0, ALU.is_ge, float(XW), ALU.mult)
+            tt(A("cn"), A("nfb"), A("AT", 0, 8), ALU.min)
+        scan(A("SC"), P(B4, B4 + 136), A("D1"), ALU.min, ALU.max)
+        copy(R("DS", t, 8), A("SC", 16, 136, 17))
+        send(far(t), R("DL", t, 8), R("DS", t, 8), "d%d" % t)
+        copy(A("cu"), R("BL", t, ZW, 128, 136))
+        ts(A("flag"), A("SC", 16, 136, 17), float(SH), ALU.is_ge)
+        tt(R("VS", t), IND(A("hmin"), A("cu")), R("BL", t, ZW, 0, 128), ALU.min)
+        send(home(t), R("VL", t), R("VS", t), "v%d" % t)
+        act(A("OHk"), IND(A("OHW"), oy), ACT.Copy)
+        if not last:
+            mm(P(B6 + 128, B6 + 256), R("ZS", t, ZW, 0, 128), A("NIb"), True, False)
+            mm(P(B6 + 128, B6 + 256), A("ykb"), A("Ib"), False, True)
+            mm(P(B5 + 64, B5 + 192), A("Ib"), A("MD", 0, 128), True, False)
+            mm(P(B5 + 64, B5 + 192), A("WB"), R("ZL", t + 1, ZW, 0, 128), False, True)
+            lnames(t + 1)
+            act(A("zT"), P(B6 + 128, B6 + 256), ACT.Abs)
+            expand(t + 1, 0, 6)
+            spass(A("NH"), "SN", True, False, range(5))
+            scan(A("su"), A("RST", 0, 128), P(B5 + 64, B5 + 192), ALU.mult, ALU.max)
+        base = A("BASE", 0, 48)
+        if t >= 4:
+            ts(A("cls"), A("cn"), float(E0), ALU.is_ge)
+        tt(A("G48"), IND(A("flag"), A("off8", 0, 3)), A("AT"), ALU.mult)
+        if t >= 4:
+            tt(A("G32"), IND(A("cls"), A("off8", 0, 2)), R("FIN", t - 4, 72, 0, 32), ALU.mult)
+            if t == 4:
+                copy(A("PB", 0, 24), A("BASE", 0, 24))
+            tt(A("PB", 24, 56), A("G32"), A("BASE", 24, 56), ALU.max)
+            base = A("PB", 0, 48)
+        if not last:
+            ts(A("uf"), A("su", 15, 128, 16), -float(MID), ALU.add)
+        tt(R("FIN", t, 72, 16, 64), A("G48"), base, ALU.max)
+        if not last:
+            ts(A("ubf"), A("uf"), 511, ALU.bitwise_and)
+        copy(R("Q", t, 56, 0, 48), R("FIN", t, 72, 16, 64))
+        if not last:
+            copy(A("bfu"), A("ubf"))
+        if t >= 4:
+            copy(R("Q", t, 56, 48, 56), A("PB", 48, 56))
+            send(far(t), R("EL", t, 8), R("Q", t, 56, 48, 56), "e%d" % t)
+        tt(A("dl"), IND(A("NDW", ndw, ndw + GW), R("Q", t, 56, 32, 40)), A("OHk"), ALU.mult)
+        if not last:
+            copy(R("MS", t + 1, ZW, 128, 136), A("bfu"))
+        tt(ccol(t), ccol(t), A("dl"), ALU.add)
+        act(A("nvf"), R("VS", t), ACT.Identity, 0.0, -1.0)
+        if not last:
+            expand(t + 1, 6, 9)
+            mprep(t + 1)
+            zpart(0)
+            zpart(1)
+        else:
+            codec(3)
+        if t < 4:
+            act(A("NDW", ndw + 16, ndw + 144), A("dl"), ACT.Identity, 0.0, -1.0)
+        else:
+            act(A("capf"), R("VS", t), ACT.Identity, 63.0, -1.0)
+        if t == 0:
+            iota(A("IOT", 1024, XW), [[1, XW - 1024]], 1024 - SH, 0)
+        act(A("nvh"), R("VL", t), ACT.Identity, 0.0, -1.0)
+        act(blockx(t), R("VL", t), ACT.Copy)
+        if t >= 4:
+            act(A("caph"), R("VL", t), ACT.Identity, 63.0, -1.0)
+        if not last:
+            expand(t + 1, 9, 16)
+        else:
+            records(t)
+        steps = [(R("DL", t, 8), R("VS", t), ALU.max, A("nvf")), (R("Q", t, 56, 24, 32), R("VL", t), ALU.max, A("nvh"))]
+        if t >= 4:
+            steps += [(R("Q", t, 56, 40, 48), A("caph"), ALU.min, R("VL", t)), (R("EL", t, 8), A("capf"), ALU.min, R("VS", t))]
+        for off, lim, op, add in steps:
+            tt(A("tk"), IND(xw, off), lim, op)
+            tt(IND(xw, off), A("tk"), add, ALU.add)
 
-    dma("G", (T.xo[:, 0:3968], []), A("X", 0, 3968), "outg")
-    lists(NR - 1)
-    entries(NR - 1)
-    records(NR - 1)
-    dma("G", (T.xo[:, 3968:4096], []), A("X", 3968, 4096), "outg")
-    ts(A("cni"), A("CN"), HALF, ALU.add)
-    ts(A("cnj"), A("cni"), 4095, ALU.bitwise_and)
-    copy(A("cnt"), A("cnj"))
+    last0 = E0 + 128 * (NR - 1)
+    dma("Y", (T.xo[:, 0:last0 - SH], []), A("X", SH, last0), "outs")
+    mask(NR - 1)
+    dma("S", (T.co[:], []), A("cnt"), "outs")
     for j in range(3):
-        dma("Y", (T.rec[8 * j:8 * j + 8, :], []), A("REC", 1024 * j, 1024 * j + 1024, p=slice(0, 128, 16)), "outs")
-    dma("Y", (T.co[:], []), A("cnt"), "outs")
+        dma("S", (T.rec[8 * j:8 * j + 8, :], []), A("REC", 1024 * j, 1024 * j + 1024, p=slice(0, 128, 16)), "outs")
+    dma("S", (T.xo[:, last0 - SH:4096], []), blockx(NR - 1), "outs")
 
     value = {}
     for q in marked:
@@ -630,5 +671,4 @@ def rank_program(g, core, T, topo):
         elif tok[0] != "sent":
             ins.then_inc(T.sem[tok[0]], 16)
     g.wait_ge(T.sem["sent"], sent[0])
-    g.wait_ge(T.sem["outg"], dmacount["outg"])
     g.sync.wait_ge(T.sem["outs"], dmacount["outs"])

from concourse.mybir import AluOpType, AxisListType, ActivationFunctionType

ALU = AluOpType
ACT = ActivationFunctionType
NR = 8
WT = [1, 64, 5, 83, 17, 131, 29, 211, 43, 157, 61, 239, 71, 113, 97, 199]
GW = 272
SW = 8 * GW
SH = 128
E0 = SH + 3072
XW = SH + 4096
MID = SH + 2048
ZW = 144
ROUND = 12582912.0
HALF = 4095.5
BIG = 16384.0
HUGE = 1073741824.0


def sb(cols, dtype):
    return ("sbuf", [128, cols], dtype)


F32, BF, F16, I32, U16 = "float32", "bfloat16", "float16", "int32", "uint16"
SCRATCH = {
    "ps": ("psum", [128, 4096], F32),
    "X": sb(XW, BF), "NT": sb(E0, BF), "NW": sb(8192, BF), "fri": sb(192, I32), "frb": sb(192, BF),
    "pli": sb(512, I32), "plu": sb(512, U16), "CN": sb(512, F32), "cnt": sb(512, F32), "b0i": sb(8, I32), "IOT": sb(XW, F32),
    "ZS": sb(NR * ZW, BF), "ZL": sb(NR * ZW, BF), "NS": sb(NR * 128, BF), "NL": sb(NR * 128, BF),
    "MS": sb(NR * ZW, F16), "ML": sb(NR * ZW, F16), "HS": sb(NR * 128, F16), "HL": sb(NR * 128, F16),
    "BS": sb(NR * ZW, F32), "BL": sb(NR * ZW, F32), "VS": sb(NR * 128, BF), "VL": sb(NR * 128, BF),
    "DS": sb(NR * 8, U16), "DL": sb(NR * 8, U16), "EL": sb(NR * 8, U16), "Q": sb(NR * 56, U16), "FIN": sb(NR * 72, F32),
    "zxf": sb(2048, BF), "ybuf": sb(2048, BF), "rbuf": sb(2048, BF), "hmin": sb(4096, BF), "OHW": sb(4096, BF),
    "EXP": sb(2048, BF), "SK": sb(SW, BF), "SN": sb(SW, BF), "SL": sb(SW, BF),
    "SG": sb(1024, BF), "TR": sb(512, BF), "EC": sb(1024, BF), "AB": sb(512, BF),
    "EM": ("sbuf", [128, 64, 16], BF), "REC": sb(3072, F32),
    "KI": sb(GW, F32), "LI": sb(GW, F32), "CI": sb(GW, F32), "GI": sb(128, F32),
    "KP": sb(GW, BF), "KN": sb(GW, BF), "LP": sb(GW, BF), "KA": sb(GW, BF), "KB": sb(GW, BF), "CR": sb(GW, BF),
    "pint": sb(16, I32), "col": sb(32, F32), "blk": sb(8, F32), "blkA": sb(8, F32), "blkb": sb(8, BF), "BS8": sb(8, F32),
    "I16": sb(16, F32), "Zw": sb(144, BF), "Zn": sb(144, BF), "BLK": sb(128, BF), "WB": sb(128, BF),
    "MD": sb(256, BF), "RST": sb(256, F32), "sc": sb(256, F32), "su": sb(128, F32),
    "Ib": sb(128, BF), "NIb": sb(128, BF), "I32": sb(128, F32), "I128": sb(128, BF), "CIb": sb(128, BF),
    "uf": sb(8, I32), "ubf": sb(8, I32), "wrow": sb(16, F32), "wtmp": sb(16, F32),
    "off8": sb(4, U16), "JC": sb(16, F32), "iG": sb(8, F32), "BASE": sb(56, F32), "PB": sb(56, F32), "AT": sb(48, F32),
    "G48": sb(48, F32), "G32": sb(32, F32), "PRE": sb(136, F32), "D1": sb(136, F32), "SC": sb(136, F32), "T2": sb(GW, BF),
    "NDW": sb(4 * GW, F32), "Li": sb(128, I32), "La": sb(128, I32), "Lr": sb(128, F32), "Lu": sb(256, U16), "L16": sb(256, F16),
    "NH": sb(128, BF), "Mi": sb(128, I32), "Ma": sb(128, I32), "Mr": sb(128, F32), "Mu": sb(128, U16),
    "bfu": sb(8, U16), "FT": sb(256, F16), "U": sb(8, F32), "UX": sb(128, F32), "Ui": sb(8, I32), "dec": sb(16, I32),
    "OF": sb(16, U16), "LM": sb(256, F16), "r1": sb(8, BF), "r2": sb(16, BF), "cm": sb(16, F32),
    "nfb": sb(8, F32), "cn": sb(8, F32), "cls": sb(8, F32), "flag": sb(8, F32), "cu": sb(8, U16), "ykb": sb(128, BF),
    "zT": sb(128, BF), "bu": sb(8, U16), "nv": sb(128, BF), "OHk": sb(128, F32),
    "dl": sb(128, F32), "tk": sb(128, BF), "nvf": sb(128, BF), "nvh": sb(128, BF), "capf": sb(128, BF), "caph": sb(128, BF),
}
MSGS = ["z", "n", "m", "h", "y", "v", "d", "e"]
SEMAPHORES = (["V", "S", "P", "G", "sent", "ld0", "ld1", "ld2", "ld3", "ld4", "ld5", "ldx", "outs"]
              + [m + str(t) for m in MSGS for t in range(NR)])


def rank_program(g, core, T, topo):
    rank = T.rank_of(core)
    if rank is None:
        return
    n = len(T.cores)
    queues = {"V": g.vector, "S": g.scalar, "P": g.tensor, "G": g, "Y": g.sync}

    ops = []
    hist = {}
    clock = {q: {} for q in queues}
    seq = {q: 0 for q in queues}
    marked = {q: set() for q in queues if q != "Y"}

    def A(name, lo=0, hi=None, step=1, p=None):
        t = T[name]
        if hi is None:
            hi = t.shape[-1]
        ps_ = slice(None) if p is None else p
        ap_ = t[ps_, lo:hi] if step == 1 else t[ps_, lo:hi:step]
        return (ap_, [(name, lo, hi, step)])

    def IND(win, off):
        return (win[0].indirect(off[0]), win[1], off[1])

    def P(lo, hi, step=1, p=None):
        return A("ps", lo, hi, step, p)

    def keys(x):
        return x[1] if isinstance(x, tuple) else []

    def ap(x):
        return x[0] if isinstance(x, tuple) else x

    def record(q, fn, reads, writes, token=None):
        need = {}
        snaps = []
        for lst, wr in ((reads, False), (writes, True)):
            for (name, lo, hi, st) in lst:
                for e in hist.get(name, []):
                    elo, ehi, ewr, eq, tok, snap, est = e
                    over = elo < hi and lo < ehi and not (st == est and (lo - elo) % st)
                    if name == "ps" and eq != q:
                        dep = elo // 512 <= (hi - 1) // 512 and lo // 512 <= (ehi - 1) // 512
                    elif eq == q and q == "P":
                        dep = False
                    else:
                        dep = over and (ewr or wr)
                    if dep and clock[q].get(tok[0], 0) < tok[1]:
                        if need.get(tok[0], 0) < tok[1]:
                            need[tok[0]] = tok[1]
                        snaps.append((tok, snap))
        for tok, snap in snaps:
            for k2, v2 in snap.items():
                if k2 != tok[0] and need.get(k2, 1 << 30) <= v2:
                    need.pop(k2)
        for tok, snap in snaps:
            for k2, v2 in snap.items():
                if clock[q].get(k2, 0) < v2:
                    clock[q][k2] = v2
        for k2, v2 in need.items():
            if clock[q].get(k2, 0) < v2:
                clock[q][k2] = v2
            if k2 in marked:
                marked[k2].add(v2)
        if token is None:
            seq[q] += 1
            tok, eq = (q, seq[q]), q
        else:
            tok, eq = token, "dma"
        snap = dict(clock[q])
        ops.append((q, fn, need, tok, token is None))

        def covers(lo, hi, st, e):
            return lo <= e[0] and e[1] <= hi and (st == 1 or (st == e[6] and (lo - e[0]) % st == 0))

        for (name, lo, hi, st) in writes:
            h = hist.setdefault(name, [])
            h[:] = [e for e in h if not covers(lo, hi, st, e)]
            h.append((lo, hi, True, eq, tok, snap, st))
        for (name, lo, hi, st) in reads:
            h = hist.setdefault(name, [])
            h[:] = [e for e in h if not (e[3] == eq and eq != "dma" and not e[2] and covers(lo, hi, st, e))]
            h.append((lo, hi, False, eq, tok, snap, st))

    def rw(out, ins):
        r = []
        for x in ins:
            r += keys(x)
            if isinstance(x, tuple) and len(x) == 3:
                r += x[2]
        if len(out) == 3:
            r += out[2]
        return r, out[1]

    def copy(out, in_):
        record("V", lambda: g.vector.tensor_copy(ap(out), ap(in_)), *rw(out, [in_]))

    def tt(out, a, b, op):
        record("V", lambda: g.vector.tensor_tensor(ap(out), ap(a), ap(b), op), *rw(out, [a, b]))

    def ts(out, a, s1, op0, s2=None, op1=None):
        if op1 is None:
            record("V", lambda: g.vector.tensor_scalar(ap(out), ap(a), ap(s1), None, op0), *rw(out, [a, s1]))
        else:
            record("V", lambda: g.vector.tensor_scalar(ap(out), ap(a), ap(s1), ap(s2), op0, op1), *rw(out, [a, s1, s2]))

    def mset(out, c):
        record("V", lambda: g.vector.memset(ap(out), c), *rw(out, []))

    def scan(out, d0, d1, op0, op1):
        record("V", lambda: g.vector.tensor_tensor_scan(ap(out), ap(d0), ap(d1), 0.0, op0, op1), *rw(out, [d0, d1]))

    def red(out, in_, op, absv):
        record("V", lambda: g.vector.tensor_reduce(ap(out), ap(in_), AxisListType.X, op, apply_absolute_value=absv),
               *rw(out, [in_]))

    def act(out, in_, func=ACT.Identity, bias=0.0, scale=1.0):
        record("S", lambda: g.scalar.activation(ap(out), ap(in_), func, bias=ap(bias), scale=ap(scale)),
               *rw(out, [in_, bias, scale]))

    def mm(out, lhsT, rhs, start, stop):
        record("P", lambda: g.tensor.matmul(ap(out), ap(lhsT), ap(rhs), start, stop), *rw(out, [lhsT, rhs]))

    def iota(out, pattern, base, cm, flt=True):
        if flt:
            record("G", lambda: g.iota(ap(out), pattern, base, cm, allow_small_or_imprecise_dtypes=True), *rw(out, []))
        else:
            record("G", lambda: g.iota(ap(out), pattern, base, cm), *rw(out, []))

    dmacount = {}

    def dma(q, out, in_, sem):
        dmacount[sem] = dmacount.get(sem, 0) + 16
        record(q, lambda: queues[q].dma_start(ap(out), ap(in_)), keys(in_), keys(out), token=(sem, dmacount[sem]))

    sent = [0]

    def send(dst_rank, out, in_, sem):
        dst = T.cores[dst_rank]
        rid, pid, _se = topo.addr(dst)
        sent[0] += len(topo.engines(core, dst))
        record("G", lambda: g.remote_dma(ap(out), ap(in_), T.sem[sem], T.sem["sent"], pid, rid, topo.mask(core, dst)),
               keys(in_), [], token=("sent", 0))

    def arrive(src_rank, land, sem):
        tok = (sem, len(topo.engines(T.cores[src_rank], core)))
        for (name, lo, hi, st) in land[1]:
            hist.setdefault(name, []).append((lo, hi, True, "dma", tok, {}, st))

    def far(t):
        return (rank + 1 + t % 4) % n

    def home(t):
        return (rank - 1 - t % 4) % n

    def R(name, t, w=128, lo=0, hi=None):
        return A(name, w * t + lo, w * t + (w if hi is None else hi))

    for t in range(NR):
        arrive(home(t), R("ZL", t, ZW, 0, 128 if t else 136), "z%d" % t)
        arrive(far(t), R("NL", t), "n%d" % t)
        arrive(far(t), R("ML", t, ZW, 0, 136), "m%d" % t)
        arrive(far(t), R("HL", t), "h%d" % t)
        arrive(home(t), R("BL", t, ZW, 0, 136), "y%d" % t)
        arrive(far(t), R("VL", t), "v%d" % t)
        arrive(home(t), R("DL", t, 8), "d%d" % t)
        if t >= 4:
            arrive(home(t), R("EL", t, 8), "e%d" % t)

    def C(j, p=None):
        return A("col", j, j + 1, p=p)

    PC, PM, PG, P6, P16, WC, WP, WN, CA, CBF, CBN, HI, LO, WE, TA = range(15)
    B4, B5, B6, B7 = 4 * 512, 5 * 512, 6 * 512, 7 * 512
    LOW, UPP = slice(0, 64), slice(64, 128)

    dma("Y", A("fri"), T.fr0[:], "ld0")
    dma("S", A("pli"), T.pl[:], "ld2")
    dma("Y", R("ZS", 0, ZW, 0, 128), T.z0[:], "ld1")
    dma("S", A("b0i"), T.b0[:], "ld3")
    iota(A("pint", 0, 4), [[0, 4]], 0, 1, False)
    iota(A("CI", 0, 256), [[1, 256]], 0, 0)
    iota(A("KI", 0, 256), [[1, 16], [0, 16]], 0, 0)
    iota(A("KI", 256, GW), [[1, 16]], 0, 0)
    iota(A("LI", 0, 256), [[0, 16], [1, 16]], 0, 0)
    iota(A("LI", 256, GW), [[0, 16]], -1, 0)
    mset(A("NT"), 0.0)
    for z_ in ("Zw", "Zn"):
        mset(A(z_), 0.0)
    ts(A("pint", 4, 5), A("pint", 0, 1), 15, ALU.bitwise_and)
    ts(A("pint", 5, 6), A("pint", 0, 1), 4, ALU.arith_shift_right)
    ts(A("pint", 6, 7), A("pint", 0, 1), 63, ALU.bitwise_and)
    ts(A("pint", 8, 12), A("pint", 0, 4), 7, ALU.bitwise_and)
    copy(C(PC), A("pint", 0, 1))
    copy(A("col", PM, P6 + 1), A("pint", 4, 7))
    copy(A("off8"), A("pint", 8, 12))
    ts(A("blk"), A("CI", 0, 8), C(PG), ALU.is_equal)
    ts(A("Ib"), A("CI", 0, 128), C(PC), ALU.is_equal)
    ts(A("Zn", 15, 143, 16), A("blk"), 8192.0, ALU.mult)
    ts(A("Zw", 15, 143, 16), A("blk"), 1.0 / 128, ALU.mult)
    ts(A("KP"), A("KI"), C(PM), ALU.is_equal, -128.0, ALU.mult)
    mset(A("KN", 256, GW), 0.0)
    mset(A("X", 0, SH), 0.0)
    ts(A("KN", 0, 256), A("KI", 0, 256), C(PM), ALU.is_equal, -128.0, ALU.mult)
    ts(A("frb"), A("fri"), -256.0, ALU.add)
    dma("Y", A("NT", SH, E0, p=slice(0, 128, 16)), A("frb"), "ld4")
    dma("Y", A("X", SH, E0), T.x0[:], "ldx")
    ts(R("ZS", 0, ZW, 128, 136), A("b0i"), -256.0, ALU.add)
    send(far(0), R("ZL", 0, ZW, 0, 136), R("ZS", 0, ZW, 0, 136), "z0")
    ts(A("LP"), A("LI"), C(PM), ALU.is_equal, -128.0, ALU.mult)
    for s4 in range(4):
        ts(A("plu", 128 * s4, 128 * s4 + 128), A("pli", s4, 512, 4), float(SH), ALU.add)
    act(A("NIb"), A("Ib"), ACT.Identity, 0.0, -1.0)
    for k in range(16):
        act(A("EXP", k, 2048, 16), A("Ib"), ACT.Copy)
    mm(P(B7, B7 + 128), R("ZS", 0, ZW, 0, 128), A("Ib"), True, True)
    act(A("zT"), P(B7, B7 + 128), ACT.Copy)
    for gg in range(6):
        act(A("SN", GW * gg, GW * gg + GW), A("KN"), ACT.Identity, 0.0, A("blk", gg, gg + 1))
    iota(A("CI", 256, GW), [[-16, 16]], -2048, 0)
    iota(A("GI"), [[1, 8], [0, 16]], 0, 0)
    iota(A("JC"), [[0, 2], [256, 8]], 0, 0)
    iota(A("iG"), [[16, 8]], 0, 0)
    iota(A("FT"), [[0, 256]], 1, 0)
    iota(A("RST"), [[0, 256]], 1, 0)
    iota(A("RST", 0, 256, 16), [[0, 16]], 0, 0)
    iota(A("T2", 0, 144), [[0, 144]], 0, 0)
    iota(A("T2", 144, GW), [[0, 128]], 1, 0)
    iota(A("BASE"), [[0, 56]], 0, 0)
    iota(A("AT", 40, 48), [[0, 8]], 0, 0)
    for e in range(16):
        iota(A("wrow", e, e + 1), [[0, 1]], WT[e], 0)
    iota(A("IOT", 0, SH), [[0, SH]], 0, 0)
    iota(A("IOT", SH, 1024), [[1, 1024 - SH]], 0, 0)
    ts(A("cnt"), A("pli"), SH - HALF, ALU.add)
    ts(A("OHW", 0, 256), A("LI", 0, 256), C(PM), ALU.is_equal)
    ts(A("OHW", 256, 512), A("LI", 0, 256), C(PM), ALU.is_equal)
    for j in range(1, 8):
        dma("Y", A("OHW", 512 * j, 512 * j + 512), A("OHW", 0, 512), "ld5")
    for gg in range(6, 8):
        ts(A("SN", GW * gg, GW * gg + GW), A("KN"), A("blk", gg, gg + 1), ALU.mult)
    for gg in range(8):
        ts(A("SL", GW * gg, GW * gg + GW), A("LP"), A("blk", gg, gg + 1), ALU.mult)
    ts(C(HI), C(PC), 64.0, ALU.is_ge)
    ts(C(LO), C(PC), 64.0, ALU.is_lt)
    ts(C(CA), C(P6), 0.0, ALU.is_equal, 1.0 / 4096, ALU.mult)
    ts(C(CBF), C(P6), 1.0, ALU.is_equal, 2016.0, ALU.mult)
    ts(C(CBN), C(P6), 1.0, ALU.is_equal, -2032.0, ALU.mult)
    ts(C(P16), C(PM), 16.0, ALU.mult)
    ts(C(WC), C(PC), -1.0, ALU.mult, 256.0, ALU.add)
    ts(C(WP), C(PC), -BIG, ALU.mult, 256.0 * BIG, ALU.add)
    ts(C(WN), C(PC), BIG, ALU.mult, -256.0 * BIG, ALU.add)
    ts(A("blkA", 0, 4), A("blk", 0, 4), C(HI), ALU.add)
    ts(A("blkA", 4, 8), A("blk", 4, 8), C(LO), ALU.add)
    mset(A("D1"), -HUGE)
    mset(A("PRE", 0, 136, 17), -HUGE)
    for t4 in range(4):
        iota(A("NDW", GW * t4, GW * t4 + 144), [[0, 144]], 0, 0)

    def fold16(buf, lo, cols, out_lo, w):
        for k in range(16):
            mm(P(out_lo, out_lo + cols), A(w, 15 - k, 143 - k), A(buf, lo + k, lo + 16 * cols, 16), k == 0, k == 15)

    def ccol(t):
        return A("CN", t % 4, 512, 4)

    def names(ch, eng):
        src = IND(A("NT"), A("plu", 64 * ch, 64 * ch + 64))
        out = A("NW", 1024 * ch, 1024 * ch + 1024)
        if eng == "S":
            act(out, src, ACT.Copy)
        else:
            copy(out, src)

    def table_constants():
        act(A("CR", 0, 256), A("CI", 0, 256), ACT.Identity, C(CBF), C(CA))
        act(A("CR", 256, GW), A("CI", 256, GW), ACT.Identity, C(CBN), C(CA))

    def late_constants():
        act(A("KA", p=LOW), A("KP", p=LOW), ACT.Copy)
        act(A("KB", p=UPP), A("KP", p=UPP), ACT.Copy)
        act(A("KA", p=UPP), A("CR", p=UPP), ACT.Copy)
        act(A("KB", p=LOW), A("CR", p=LOW), ACT.Copy)
        for gg in range(8):
            act(A("SK", GW * gg, GW * gg + GW), A("KA" if gg < 4 else "KB"), ACT.Identity, 0.0, A("blkA", gg, gg + 1))
        ts(A("I16"), A("CI", 0, 16), C(PM), ALU.is_equal)
        ts(A("BS8"), A("blk"), 4096.0, ALU.mult)
        ts(A("TR", 0, 128), A("CI", 0, 128), C(PC), ALU.is_lt, 0.5, ALU.mult)
        ts(A("iG"), A("iG"), C(PM), ALU.add)
        ts(A("BLK"), A("GI"), C(PG), ALU.is_equal)
        tt(A("wtmp"), A("wrow"), A("I16"), ALU.mult)
        ts(A("JC"), A("JC"), C(P16), ALU.add)
        ts(A("G48", 0, 8), A("iG"), BIG, ALU.mult, 8192.0 - 256 * BIG - HUGE, ALU.add)
        ts(A("G48", 8, 16), A("iG"), -BIG, ALU.mult, 8192.0 + 256 * BIG - HUGE, ALU.add)
        red(C(WE), A("wtmp"), ALU.add, False)
        act(A("I128"), A("Ib"), ACT.Identity, 0.0, 128.0)
        act(A("CIb"), A("CI", 0, 128), ACT.Copy)
        for j in range(1, 4):
            act(A("TR", 128 * j, 128 * j + 128), A("TR", 0, 128), ACT.Copy)
        act(A("I32"), A("Ib"), ACT.Copy)
        act(A("MD"), A("OHW", 0, 256), ACT.Identity, -131072.0, 131072.0 + MID)
        act(A("blkb"), A("blk"), ACT.Copy)
        for gg in range(8):
            for h in range(2):
                act(A("PRE", 1 + 8 * h + gg, 136, 17), A("G48", 8 * h, 8 * h + 8), ACT.Identity, HUGE, A("blk", gg, gg + 1))
        for gg in range(8):
            act(A("SG", 128 * gg, 128 * gg + 128), A("Ib"), ACT.Identity, A("blk", gg, gg + 1), 0.0)
        act(A("WB"), A("BLK"), ACT.Identity, 0.0, C(WE))
        for o in (24, 40, 48):
            act(A("BASE", o, o + 8), A("iG"), ACT.Copy)
        act(A("D1", 16, 136, 17), A("iG"), ACT.Copy)
        act(A("AT", 32, 40), A("iG"), ACT.Identity, 144.0, 1.0)
        for t4 in range(4):
            act(A("FIN", 72 * t4 + 8, 72 * t4 + 16), A("iG"), ACT.Identity, 16.0, 1.0)

    banks = [(0, 512), (512, 1024), (1024, 1536), (1536, 2048), (2048, SW)]

    def spass(lhsT, sel, start, stop, which):
        for b in which:
            lo, hi = banks[b]
            mm(P(lo, hi), lhsT, A(sel, lo, hi), start, stop)

    def kpass(b):
        lo, hi = banks[b]
        cut = 4 * GW
        for a_, b_, j in ((lo, min(hi, cut), 0), (max(lo, cut), hi, 1)):
            if a_ < b_:
                mm(P(a_, b_), A("FT", 128 * j, 128 * j + 128), A("SK", a_, b_), False, False)

    def lnames(t):
        act(A("Lr"), ccol(t), ACT.Identity, ROUND, 1.0 / 8192)
        act(A("NH"), A("Lr"), ACT.Identity, 64.0 * ROUND, -64.0)

    def lprep(t):
        ts(A("Li"), ccol(t), HALF, ALU.add)
        ts(A("La"), A("Li"), 8191, ALU.bitwise_and)
        copy(R("Lu", t % 2), A("La"))
        ts(R("L16", t % 2), R("Lu", t % 2), -float(MID), ALU.add)

    def mprep(t):
        ts(A("Mi"), IND(A("CN"), A("bfu")), HALF, ALU.add)
        mnames(t)
        ts(A("Ma"), A("Mi"), 8191, ALU.bitwise_and)
        copy(A("Mu"), A("Ma"))
        ts(R("MS", t, ZW, 0, 128), A("Mu"), -float(MID), ALU.add)
        send(home(t), R("ML", t, ZW, 0, 136), R("MS", t, ZW, 0, 136), "m%d" % t)

    def mnames(t):
        act(A("Mr"), IND(A("CN"), A("bfu")), ACT.Identity, ROUND, 1.0 / 8192)
        act(R("NS", t), A("Mr"), ACT.Identity, -64.0 * ROUND, 64.0)
        send(home(t), R("NL", t), R("NS", t), "n%d" % t)

    def expand(t, k0=0, k1=16):
        for k in range(k0, k1):
            act(A("zxf", k, 2048, 16), R("ZL", t, ZW, 0, 128), ACT.Copy)

    def codec(s4):
        ts(A("fri", 0, 128), ccol(s4), HALF, ALU.add)
        ts(A("pli", 0, 128), A("fri", 0, 128), 8191, ALU.bitwise_and)
        ts(A("cnt", s4, 512, 4), A("pli", 0, 128), -float(SH), ALU.add)

    def records(t):
        for j, o in ((0, 16), (1, 0), (2, 8)):
            act(A("REC", 1024 * j + 128 * t, 1024 * j + 128 * t + 128), IND(A("IOT"), R("Q", t, 56, o, o + 8)), ACT.Copy)

    def blockx(t):
        return A("X", E0 + 128 * t, E0 + 128 * t + 128)

    def mask(t):
        tt(blockx(t), IND(A("T2"), R("Q", t, 56, 32, 40)), blockx(t), ALU.mult)

    def zpart(c):
        b = B5 + 512 * (c % 2)
        mm(P(b, b + 512), A("zT"), A("EXP", 512 * c, 512 * c + 512), True, True)

    def ygather(t, c):
        yw = E0 + 128 * max(0, t - 3)
        act(A("ybuf", 1024 * c, 1024 * c + 1024), IND(A("X", 0, yw), R("Lu", t % 2, 128, 64 * c, 64 * c + 64)), ACT.Copy)

    def ymin(c):
        b = B5 + 512 * (c % 2)
        tt(A("rbuf", 512 * c, 512 * c + 512), A("ybuf", 512 * c, 512 * c + 512), P(b, b + 512), ALU.min)

    def emrows(gg):
        return (T.EM[:, gg:64:8, :], [("EM", gg, gg + 1, 1)])

    for ch, eng in enumerate("VSVSVVSV"):
        names(ch, eng)
        if ch == 3:
            expand(0)
            ts(A("bfu"), R("ZL", 0, ZW, 128, 136), 256.0, ALU.add)
            ts(A("Mu"), IND(A("pli"), A("bfu")), float(SH), ALU.add)
            copy(R("MS", 0, ZW, 128, 136), A("bfu"))
            ts(R("MS", 0, ZW, 0, 128), A("Mu"), -float(MID), ALU.add)
            send(home(0), R("ML", 0, ZW, 0, 136), R("MS", 0, ZW, 0, 136), "m0")
            copy(R("Lu", 0), A("plu", 0, 128))
            ts(R("L16", 0), A("plu", 0, 128), -float(MID), ALU.add)
        if ch % 2:
            s4 = ch // 2
            fold16("NW", 2048 * s4, 128, 512 * s4, "Zn")
    zpart(0)
    zpart(1)
    for s4 in range(4):
        tt(ccol(s4), P(512 * s4, 512 * s4 + 128), A("cnt", s4, 512, 4), ALU.add)
    mnames(0)
    lnames(0)
    spass(A("NH"), "SN", True, False, range(5))
    table_constants()

    for t in range(NR):
        xw = A("X", 0, E0 + 128 * t)
        last = t == NR - 1
        for h in range(2):
            tt(A("hmin", 1024 * h, 1024 * h + 1024), IND(xw, A("Mu", 64 * h, 64 * h + 64)), A("zxf", 1024 * h, 1024 * h + 1024), ALU.min)
        for c in range(2):
            ygather(t, c)
        if t > 0:
            spass(R("NL", t), "SL", False, False, range(5))
        fold16("hmin", 0, 64, B7, "Zw")
        fold16("hmin", 1024, 64, B7 + 64, "Zw")
        ymin(0)
        ymin(1)
        zpart(2)
        zpart(3)
        copy(R("HS", t), P(B7, B7 + 128))
        send(home(t), R("HL", t), R("HS", t), "h%d" % t)
        ymin(2)
        ymin(3)
        fold16("rbuf", 0, 64, B7 + 128, "Zw")
        fold16("rbuf", 1024, 64, B7 + 192, "Zw")
        if t == 0:
            spass(R("NL", t), "SL", False, False, range(5))
            late_constants()
            iota(A("hmin", 2048, 4096), [[0, 2048]], 63, 0)
        else:
            mask(t - 1)
            records(t - 1)
        ts(A("AT", 16, 24), R("ML", t, ZW, 128, 136), float(SH), ALU.add)
        copy(A("bu"), R("ML", t, ZW, 128, 136))
        if not last:
            lprep(t + 1)
        if t > 4:
            codec(t - 5)
        copy(A("FT", 0, 128, p=LOW), P(B7 + 128, B7 + 256, p=LOW))
        copy(A("FT", 128, 256, p=UPP), P(B7 + 128, B7 + 256, p=UPP))
        for b in range(5):
            kpass(b)
            spass(R("HL", t), "SL", False, True, (b,))
        ndw = GW * (t % 4)
        act(A("nv"), IND(A("IOT", SH, SH + 512), A("bu")), ACT.Identity, -256.0 * 64, 64.0)
        reg = P(B6 + 256, B6 + 384)
        mm(reg, A("I128"), A("NH"), True, False)
        mm(reg, A("Ib"), A("CIb"), False, False)
        mm(reg, A("NIb"), R("L16", t % 2), False, False)
        mm(reg, A("I128"), A("nv"), False, True)
        for gg in range(8):
            red(A("U", gg, gg + 1), P(GW * gg, GW * gg + GW), ALU.min, True)
            if gg < 7:
                act(A("UX", 16 * gg, 16 * gg + 16), A("I16"), ACT.Identity, 0.0, A("U", gg, gg + 1))
            if gg == 4:
                act(A("NDW", ndw + 144, ndw + GW), reg, ACT.Identity, float(E0 + 128 * t - MID), 1.0)
        mm(P(0, 512), A("Ib"), A("TR"), True, False)
        ts(A("UX", 112, 128), A("I16"), A("U", 7, 8), ALU.mult)
        mm(P(B5, B5 + 8), A("UX"), A("BS8"), True, True)
        for b in (512, 1024, 1536):
            mm(P(b, b + 512), A("Ib"), A("TR"), True, False)
        mm(P(B7 + 256, B7 + 512), A("Ib"), A("MD"), True, False)
        mm(P(B4, B4 + 136), A("I32"), A("PRE"), True, False)
        ts(A("r1"), A("U"), 2017.0, ALU.is_lt, C(WC), ALU.mult)
        copy(A("Ui"), P(B5, B5 + 8))
        ts(A("dec", 8, 16), A("Ui"), 4, ALU.logical_shift_right, 15, ALU.bitwise_and)
        ts(A("dec", 0, 8), A("Ui"), 0x80F, ALU.bitwise_and)
        tt(R("BS", t, ZW, 128, 144), A("dec"), A("JC"), ALU.add)
        copy(A("OF"), R("BS", t, ZW, 128, 144))
        oy, ol = A("OF", 8, 16), A("OF", 0, 8)
        act(R("BS", t, ZW, 0, 128), IND(A("ybuf"), oy), ACT.Copy)
        send(far(t), R("BL", t, ZW, 0, 136), R("BS", t, ZW, 0, 136), "y%d" % t)
        lc, lm = A("LM", 0, 128), A("LM", 128, 256)
        tt(lc, IND(A("OHW"), oy), R("L16", t % 2), ALU.mult)
        tt(lm, IND(A("OHW"), ol), R("ML", t, ZW, 0, 128), ALU.mult)
        if not last:
            act(A("ykb"), R("BS", t, ZW, 0, 128), ACT.Copy)
            mm(P(B6, B6 + 128), A("NIb"), R("ZS", t, ZW, 0, 128), True, False)
        mm(P(B5 + 16, B5 + 24), lc, A("blkb"), True, True)
        if not last:
            mm(P(B6, B6 + 128), A("Ib"), A("ykb"), False, True)
        mm(P(B5 + 24, B5 + 32), lm, A("blkb"), True, True)
        for gg in range(8):
            mm(P(256 * gg, 256 * gg + 256), A("SG", 128 * gg, 128 * gg + 128), A("LM"), False, gg % 2 == 1)
        mm(P(B7 + 256, B7 + 512), A("BLK"), A("LM"), False, True)
        copy(A("cm"), P(B5 + 16, B5 + 32))
        if not last:
            act(R("ZS", t + 1, ZW, 0, 128), P(B6, B6 + 128), ACT.Abs)
            send(far(t + 1), R("ZL", t + 1, ZW, 0, 128), R("ZS", t + 1, ZW, 0, 128), "z%d" % (t + 1))
        for gg in range(8):
            ts(A("EC", 128 * gg, 128 * gg + 128), P(256 * gg, 256 * gg + 128), A("cm", gg, gg + 1), ALU.is_equal)
        for g0 in (0, 2):
            for gg in (g0, g0 + 1):
                act(A("AB", 128 * gg, 128 * gg + 128), P(256 * gg + 128, 256 * gg + 256), ACT.Abs, A("cm", 8 + gg, 9 + gg), -1.0)
            for gg in (g0, g0 + 1):
                act(emrows(gg), A("AB", 128 * gg, 128 * gg + 128), ACT.Relu, 1.0, -2.0)
        for gg in range(8):
            mm(P(B5 + 32 + gg, B5 + 33 + gg), A("EC", 128 * gg, 128 * gg + 128), A("r1", gg, gg + 1), True, True)
        scan(A("sc"), A("RST"), P(B7 + 256, B7 + 512), ALU.mult, ALU.max)
        for gg in (6, 7):
            ts(emrows(gg), P(256 * gg + 128, 256 * gg + 256), A("cm", 8 + gg, 9 + gg), ALU.is_equal)
        ts(A("r2", 0, 8), P(B5 + 32, B5 + 40), C(WC), ALU.is_equal, C(WP), ALU.mult)
        ts(A("r2", 8, 16), P(B5 + 32, B5 + 40), C(WC), ALU.is_equal, C(WN), ALU.mult)
        for gg in (4, 5):
            ts(emrows(gg), P(256 * gg + 128, 256 * gg + 256), A("cm", 8 + gg, 9 + gg), ALU.is_equal)
        cg, mg = A("sc", 15, 128, 16), A("sc", 143, 256, 16)
        act(A("D1", 0, 136, 17), mg, ACT.Copy)
        act(A("AT", 0, 16), A("sc", 15, 256, 16), ACT.Copy)
        act(A("AT", 24, 32), cg, ACT.Copy)
        if t >= 4:
            act(R("FIN", t - 4, 72, 0, 8), cg, ACT.Copy)
        for j in range(8):
            mm(P(B4 + 17 * j + 1, B4 + 17 * j + 17), (T.EM[:, 8 * j:8 * j + 8, :], [("EM", 0, 8, 1)]), A("r2"), False, j == 7)
        if t >= 4:
            ts(A("nfb"), R("BS", t, ZW, 128, 136), 2048.0, ALU.is_ge, float(XW), ALU.mult)
            tt(A("cn"), A("nfb"), A("AT", 0, 8), ALU.min)
        scan(A("SC"), P(B4, B4 + 136), A("D1"), ALU.min, ALU.max)
        copy(R("DS", t, 8), A("SC", 16, 136, 17))
        send(far(t), R("DL", t, 8), R("DS", t, 8), "d%d" % t)
        copy(A("cu"), R("BL", t, ZW, 128, 136))
        ts(A("flag"), A("SC", 16, 136, 17), float(SH), ALU.is_ge)
        tt(R("VS", t), IND(A("hmin"), A("cu")), R("BL", t, ZW, 0, 128), ALU.min)
        send(home(t), R("VL", t), R("VS", t), "v%d" % t)
        act(A("OHk"), IND(A("OHW"), oy), ACT.Copy)
        if not last:
            mm(P(B6 + 128, B6 + 256), R("ZS", t, ZW, 0, 128), A("NIb"), True, False)
            mm(P(B6 + 128, B6 + 256), A("ykb"), A("Ib"), False, True)
            mm(P(B5 + 64, B5 + 192), A("Ib"), A("MD", 0, 128), True, False)
            mm(P(B5 + 64, B5 + 192), A("WB"), R("ZL", t + 1, ZW, 0, 128), False, True)
            lnames(t + 1)
            act(A("zT"), P(B6 + 128, B6 + 256), ACT.Abs)
            expand(t + 1, 0, 6)
            spass(A("NH"), "SN", True, False, range(5))
            scan(A("su"), A("RST", 0, 128), P(B5 + 64, B5 + 192), ALU.mult, ALU.max)
        base = A("BASE", 0, 48)
        if t >= 4:
            ts(A("cls"), A("cn"), float(E0), ALU.is_ge)
        tt(A("G48"), IND(A("flag"), A("off8", 0, 3)), A("AT"), ALU.mult)
        if t >= 4:
            tt(A("G32"), IND(A("cls"), A("off8", 0, 2)), R("FIN", t - 4, 72, 0, 32), ALU.mult)
            if t == 4:
                copy(A("PB", 0, 24), A("BASE", 0, 24))
            tt(A("PB", 24, 56), A("G32"), A("BASE", 24, 56), ALU.max)
            base = A("PB", 0, 48)
        if not last:
            ts(A("uf"), A("su", 15, 128, 16), -float(MID), ALU.add)
        tt(R("FIN", t, 72, 16, 64), A("G48"), base, ALU.max)
        if not last:
            ts(A("ubf"), A("uf"), 511, ALU.bitwise_and)
        copy(R("Q", t, 56, 0, 48), R("FIN", t, 72, 16, 64))
        if not last:
            copy(A("bfu"), A("ubf"))
        if t >= 4:
            copy(R("Q", t, 56, 48, 56), A("PB", 48, 56))
            send(far(t), R("EL", t, 8), R("Q", t, 56, 48, 56), "e%d" % t)
        tt(A("dl"), IND(A("NDW", ndw, ndw + GW), R("Q", t, 56, 32, 40)), A("OHk"), ALU.mult)
        if not last:
            copy(R("MS", t + 1, ZW, 128, 136), A("bfu"))
        tt(ccol(t), ccol(t), A("dl"), ALU.add)
        act(A("nvf"), R("VS", t), ACT.Identity, 0.0, -1.0)
        if not last:
            expand(t + 1, 6, 9)
            mprep(t + 1)
            zpart(0)
            zpart(1)
        else:
            codec(3)
        if t < 4:
            act(A("NDW", ndw + 16, ndw + 144), A("dl"), ACT.Identity, 0.0, -1.0)
        else:
            act(A("capf"), R("VS", t), ACT.Identity, 63.0, -1.0)
        if t == 0:
            iota(A("IOT", 1024, XW), [[1, XW - 1024]], 1024 - SH, 0)
        act(A("nvh"), R("VL", t), ACT.Identity, 0.0, -1.0)
        act(blockx(t), R("VL", t), ACT.Copy)
        if t >= 4:
            act(A("caph"), R("VL", t), ACT.Identity, 63.0, -1.0)
        if not last:
            expand(t + 1, 9, 16)
        else:
            records(t)
        steps = [(R("DL", t, 8), R("VS", t), ALU.max, A("nvf")), (R("Q", t, 56, 24, 32), R("VL", t), ALU.max, A("nvh"))]
        if t >= 4:
            steps += [(R("Q", t, 56, 40, 48), A("caph"), ALU.min, R("VL", t)), (R("EL", t, 8), A("capf"), ALU.min, R("VS", t))]
        for off, lim, op, add in steps:
            tt(A("tk"), IND(xw, off), lim, op)
            tt(IND(xw, off), A("tk"), add, ALU.add)

    last0 = E0 + 128 * (NR - 1)
    dma("Y", (T.xo[:, 0:last0 - SH], []), A("X", SH, last0), "outs")
    mask(NR - 1)
    dma("S", (T.co[:], []), A("cnt"), "outs")
    for j in range(3):
        dma("S", (T.rec[8 * j:8 * j + 8, :], []), A("REC", 1024 * j, 1024 * j + 1024, p=slice(0, 128, 16)), "outs")
    dma("S", (T.xo[:, last0 - SH:4096], []), blockx(NR - 1), "outs")

    value = {}
    for q in marked:
        for j, s in enumerate(sorted(marked[q])):
            value[(q, s)] = j + 1
    for q, fn, need, tok, compute in ops:
        for k2, v2 in need.items():
            queues[q].wait_ge(T.sem[k2], value[(k2, v2)] if k2 in marked else v2)
        ins = fn()
        if compute:
            if tok in value:
                ins.then_inc(T.sem[q], 1)
        elif tok[0] != "sent":
            ins.then_inc(T.sem[tok[0]], 16)
    g.wait_ge(T.sem["sent"], sent[0])
    g.sync.wait_ge(T.sem["outs"], dmacount["outs"])
